import numpy as np, ml_dtypes
CORES = [1,5,17,21,33,37,49,53]
N = 8
BF = ml_dtypes.bfloat16
V, P, Q, RO, TS = 128, 2, 1, 3, 1024
M, B = 8 * N * V, V // P
def clip(a):
    return np.minimum(np.maximum(np.floor(a), -2 ** 20), 2 ** 20 - 1).astype(np.int64)
def walls(rng, base, size, gap):
    mid = base + size * (rng.random((N, 8, 16, V)) - 0.5)
    h = gap * (16 - np.arange(16)[:, None]) * 0.0625
    l = mid + h * rng.random((N, 8, 16, V)); r = mid - h * rng.random((N, 8, 16, V)); turn = rng.random((N, 8, 1, V)) < 0.25
    return clip(np.where(turn, r, l)), clip(np.where(turn, l, r))
def common(rng):
    return walls(rng, rng.integers(-2 ** 18, 2 ** 18, (N, 8, 1, V)), np.exp2(rng.integers(8, 18, (N, 8, 1, V))), 2.0 ** 17 * rng.random((N, 8, 1, V)))
def slots(rng):
    share = rng.choice(np.array([0.1, 0.4, 0.7, 0.9]), (N, 8, 2, 1, V))
    o = rng.integers(0, M, (N, 8, 16, V)); none = (rng.random((N, 8, 2, 8, V)) < share).reshape(N, 8, 16, V)
    return np.where(none, M, o)
def pack(l, r, o):
    return {"lw": np.ascontiguousarray(l.reshape(N, 128, V)).astype(np.int32), "rw": np.ascontiguousarray(r.reshape(N, 128, V)).astype(np.int32),
            "opts": np.ascontiguousarray(o.reshape(N, 128, V)).astype(np.int32)}
def setup_inputs(rng):
    l, r = common(rng)
    return pack(l, r, slots(rng))
def setup_inputs_ties(rng):
    ix = rng.integers(0, 5, (N, 8, V)); base = 65536 * np.array([0, 0, 12, 12, -13])[:, None] + 2 * rng.integers(-4, 5, (5, 1)); out = []
    for up in (rng.integers(0, 6), 0):
        prof = base + up + rng.integers(0, 2, (5, 16))
        a = prof[ix].transpose(0, 1, 3, 2)
        i = rng.integers(0, 16, (N, 8, 1, V)); d = rng.choice(np.array([-1, 1]), (N, 8, 1, V)) * (rng.random((N, 8, 1, V)) < 0.3)
        far = 65536 * (rng.random((N, 8, 1, V)) < 0.125)
        out.append(a + d * (np.arange(16)[:, None] == i) + far)
    return pack(out[0], out[1], np.where(rng.random((N, 8, 16, V)) < 0.3, M, rng.integers(0, M, (N, 8, 16, V))))
def setup_inputs_bare(rng):
    l, r = common(rng); kinds = np.zeros((7, 16), bool)
    kinds[1, :8] = True; kinds[2, 8:] = True; kinds[3] = True; kinds[4, [0, 15]] = True; kinds[5, [7, 8]] = True; kinds[6, 0] = True
    cls = rng.integers(0, 7, (N, 8, V)); cls[:, 3] = 0; cls[:, 5] = 3
    o = np.where(kinds[cls].transpose(0, 1, 3, 2), rng.integers(0, M, (N, 8, 16, V)), M)
    for g, s, e, d in ((1, 0, -2 ** 20, 1), (6, 15, 2 ** 20 - 1, -1)):
        l[:, g] = e + d * rng.integers(0, 64, (N, 16, V)); r[:, g] = e + d * rng.integers(0, 64, (N, 16, V))
        o[:, g] = M; o[:, g, s] = V * (8 * rng.integers(0, N, (N, V)) + g) + rng.integers(0, B, (N, V))
    return pack(l, r, o)
def setup_inputs_ends(rng):
    l, r = common(rng); o = slots(rng)
    o[:, ::2] = rng.choice(np.array([0, V - 1, V, 8 * V - 1, 8 * V, M - 1, M]), (N, 4, 16, V))
    o[:, 2] = rng.integers(0, M)
    own = V * np.arange(8 * N).reshape(N, 8, 1, 1) + np.arange(V)
    o[:, 1] = np.where(rng.random((N, 16, V)) < 0.5, own[:, 1], o[:, 1])
    o[:, 3, :8] = o[:, 3, :1]; o[:, 3, 8:] = o[:, 3, 8:9]
    here = 8 * V * np.arange(N)[:, None, None]; nxt = 8 * V * ((np.arange(N) + 1) % N)[:, None, None]
    o[:, 5] = nxt + rng.integers(0, 8 * V, (N, 16, V))
    o[:, 7] = np.where(o[:, 7] < M, here + rng.integers(0, 8 * V, (N, 16, V)), M)
    return pack(l, r, o)
def setup_inputs_late(rng):
    bump = rng.random((N, 8, 1, V)) < 0.0625; bump[:, 4] = False
    l = rng.integers(-2 ** 12, 2 ** 12, (16, 1)) + bump
    r = l + rng.choice(np.array([-3, 0, 3, 5001]), (16, 1))
    z = rng.integers(0, 8, (N, 8, 2, 1, V)); s = np.arange(8)[:, None]
    has = np.where(rng.random((N, 8, 2, 1, V)) < 0.4, s == z, s >= z).reshape(N, 8, 16, V)
    o = np.where(has, rng.integers(0, M, (N, 8, 16, V)), M)
    o[:, 4] = V * (8 * rng.integers(0, N, (N, 16, V)) + 4) + rng.integers(0, V, (N, 16, V))
    return pack(l, r, o)
def setup_inputs_spread(rng):
    base = rng.choice(np.array([-1.0, 1.0]), (N, 8, 1, V)) * np.exp2(20 * rng.random((N, 8, 1, V)))
    l, r = walls(rng, base, np.abs(base) * rng.random((N, 8, 1, V)), np.exp2(18 * rng.random((N, 8, 1, V))))
    e = rng.integers(1, 5, (1, 8, 1, 1))
    o = np.minimum((M * rng.random((N, 8, 16, V)) ** e).astype(np.int64), M - 1)
    share = rng.random((N, 8, 1, V)); share[rng.integers(0, N)] = 0.0
    return pack(l, r, np.where(rng.random((N, 8, 16, V)) < share, M, o))
def check_inputs(d):
    bad = []
    for k, lo, hi in (("lw", -2 ** 20, 2 ** 20 - 1), ("rw", -2 ** 20, 2 ** 20 - 1), ("opts", 0, M)):
        if np.min(d[k]) < lo or np.max(d[k]) > hi: bad.append("range of " + k)
    return bad
def world(a, last):
    w = a.reshape(N, 8, 16, V).transpose(2, 0, 1, 3).reshape(16, M).astype(np.int32)
    return np.concatenate([w, np.full((16, 1), last, np.int32)], axis=1)
def back(w):
    return np.ascontiguousarray(w[:, :M].reshape(16, N, 8, V).transpose(1, 2, 0, 3)).reshape(N, 128, V).astype(np.float32)
def inner(L, R, ix):
    return np.concatenate([R[:, ix[:8]], -L[:, ix[8:]]], axis=1)
def reference(lw, rw, opts):
    L, R, O = world(lw, 0), world(rw, 0), world(opts, M)
    temp = (TS * np.arange(16, dtype=np.int32))[:, None]; s16 = np.arange(16); left = (s16 < 8)[:, None]
    for t in range(RO):
        nL, nR, nO = L.copy(), R.copy(), O.copy()
        v = np.tile(B * (t % P) + np.arange(B), 8 * N); c = V * np.repeat(np.arange(8 * N), B) + v
        o = O[:, c]; xl, xr = L[:, c], R[:, c]; has = o < M
        u = inner(L, R, o); gone = np.zeros(o.shape, bool)
        for q in range(Q):
            p = s16 ^ (1 + (t + 3 * q) % 7); up = u[:, p]
            ge = np.all(up >= u, axis=0); eq = np.all(up == u, axis=0)
            gone = gone | (has & has[p] & ge & (~eq | (p < s16)[:, None]))
        sl = (v + t) & 7; k = O[np.where(left, 8 + sl, sl), o]
        kl, kr = L[:, k], R[:, k]; yl, yr = xl[:, None, :], xr[:, None, :]
        under = np.all((kl[:, :8] <= yl) & (kr[:, :8] <= yr), axis=0); over = np.all((kl[:, 8:] >= yl) & (kr[:, 8:] >= yr), axis=0)
        rev = (has & ~gone & (k < M) & np.concatenate([under, over], axis=0)).reshape(2, 8, -1).astype(np.int64)
        first = (rev == 1) & (np.add.accumulate(rev, axis=1) == 1)
        ch = np.where(np.any(first, axis=1), np.add.reduce(first * k.reshape(2, 8, -1), axis=1), M)
        ent = O[s16[:, None], np.repeat(ch, 8, axis=0)]
        n = np.where(has & ~gone & ~first.reshape(16, -1), o, ent); hn = n < M
        w = np.where(hn[None], inner(L, R, n), -2 ** 23)
        l = np.where(np.any(hn[:8], axis=0)[None], np.max(w[:, :8], axis=1) - temp, xl)
        r = np.where(np.any(hn[8:], axis=0)[None], temp - np.max(w[:, 8:], axis=1), xr)
        low = l < r; mid = (l + r) >> 1
        nL[:, c] = np.where(low, mid, l); nR[:, c] = np.where(low, mid, r); nO[:, c] = n
        L, R, O = nL, nR, nO
    return {"yl": back(L), "yr": back(R), "yo": back(O)}

@@ -1,0 +1,534 @@
+from concourse.bass import DstId, RemoteDMATransfer
+from concourse.mybir import AluOpType as A, ActivationFunctionType as AF
+
+EXW = ["0", "1", "2", "3"]
+EXO = ["i", "2", "3"]
+NREP = 1
+BIG = 2.0 ** 23
+MATB = (["REP%d" % p for p in range(4)] + ["YM", "E8", "GT", "ENT0", "ENT1", "KEEPN", "ANY0", "ANY1", "KX0", "KX1", "KN0", "KN1", "IB",
+        "TMN", "TMP", "ONES", "PERM64", "PERM1", "OXH0", "OXH1", "OXL0", "OXL1"]
+        + ["ICO%d" % f for f in range(6)] + ["INV%d" % f for f in range(5)])
+MATF = ["REPF%d" % p for p in range(4)] + ["CH", "SW", "NSW", "ISW", "INVF", "IF"]
+SLID = ["OWN", "OTH", "BKO", "BKX"] + ["BD%d" % d for d in range(6)]
+DELTA = [1, -1, 2, -2, 3, -3]
+
+SCRATCH = {
+    "W": ("sbuf", [128, 8200], "float32"), "OT": ("sbuf", [128, 8208], "bfloat16"),
+    "MBF": ("sbuf", [128, 128 * len(MATB)], "bfloat16"), "MFF": ("sbuf", [128, 128 * len(MATF)], "float32"),
+    "MSL": ("sbuf", [128, 144 * len(SLID)], "bfloat16"),
+    "CI": ("sbuf", [128, 16], "int32"), "CF": ("sbuf", [128, 64], "float32"),
+    "XI": ("sbuf", [128, 144], "float32"), "MI": ("sbuf", [128, 128], "int32"), "MF": ("sbuf", [128, 640], "int32"),
+    "MKI": ("sbuf", [128, 1152], "int32"), "MK": ("sbuf", [128, 1152], "bfloat16"), "RS": ("sbuf", [128, 512], "float32"),
+    "ST": ("sbuf", [128, 256], "int32"), "OI": ("sbuf", [128, 128], "int32"),
+    "FI": ("sbuf", [128, 896], "int32"), "FB": ("sbuf", [128, 896], "bfloat16"), "HB": ("sbuf", [128, 128], "bfloat16"),
+    "OF": ("sbuf", [128, 128], "float32"), "OL": ("sbuf", [128, 128], "uint16"),
+    "XE0": ("sbuf", [128, 1024], "float32"), "XE1": ("sbuf", [128, 1024], "float32"),
+    "GM": ("sbuf", [128, 1024], "bfloat16"), "KL": ("sbuf", [128, 128], "uint16"), "KC": ("sbuf", [128, 64], "float32"),
+    "HAS": ("sbuf", [128, 64], "float32"), "U": ("sbuf", [128, 1024], "float32"),
+    "VO": ("sbuf", [128, 1024], "bfloat16"), "VX": ("sbuf", [128, 1024], "bfloat16"), "C": ("sbuf", [128, 1024], "bfloat16"),
+    "R1": ("sbuf", [128, 64], "float32"), "REV": ("sbuf", [128, 64], "bfloat16"), "ND": ("sbuf", [128, 64], "float32"),
+    "NH": ("sbuf", [128, 64], "float32"), "FF": ("sbuf", [128, 64], "float32"), "FK": ("sbuf", [128, 64], "float32"),
+    "KEEP": ("sbuf", [128, 64], "bfloat16"), "OK": ("sbuf", [128, 64], "float32"), "CL": ("sbuf", [128, 64], "uint16"),
+    "E": ("sbuf", [128, 1024], "bfloat16"), "OXA": ("sbuf", [128, 128], "bfloat16"),
+    "HN": ("sbuf", [128, 64], "bfloat16"), "U5": ("sbuf", [128, 1024], "float32"), "MX": ("sbuf", [128, 1024], "float32"),
+    "OWNW": ("sbuf", [128, 128], "float32"), "M1": ("sbuf", [128, 128], "int32"), "M2": ("sbuf", [128, 128], "int32"),
+    "NF": ("sbuf", [128, 128], "float32"), "YW0": ("sbuf", [128, 128], "float32"), "YW1": ("sbuf", [128, 128], "float32"),
+    "YI": ("sbuf", [128, 64], "int32"), "YFI": ("sbuf", [128, 320], "int32"), "YFB": ("sbuf", [128, 320], "bfloat16"),
+    "YO0": ("sbuf", [128, 64], "float32"), "YO1": ("sbuf", [128, 64], "float32"),
+    "K0": ("psum", [128, 512], "float32"), "K1": ("psum", [128, 512], "float32"), "RV": ("psum", [128, 512], "float32"),
+    "DD": ("psum", [128, 512], "float32"), "YY": ("psum", [128, 512], "float32"), "NP": ("psum", [128, 512], "float32"),
+    "UP": ("psum", [128, 1024], "float32"),
+}
+for _x in EXW:
+    SCRATCH["LW" + _x] = ("sbuf", [128, 1024], "float32")
+for _x in EXO:
+    SCRATCH["LO" + _x] = ("sbuf", [128, 2048 if _x == "i" else 1024], "bfloat16")
+SEMAPHORES = (["sV", "sS", "sP", "sG", "dOI", "dST"]
+              + [k + "W" + x for x in EXW for k in ("p", "m", "l", "f")] + [k + "O" + x for x in EXO for k in ("p", "m", "l", "f")]
+              + ["dW%s%d" % (x, h) for x in EXW for h in (0, 1)] + ["dY0", "dY1", "dO0", "dO1"])
+
+
+def rank_program(g, core, T, topo):
+    rank = T.rank_of(core)
+    if rank is None:
+        return
+    cores = list(T.cores)
+    side = [int(topo.die(c) != topo.die(cores[0])) for c in cores]
+    slot = [4 * side[r] + sum(1 for q in range(r) if side[q] == side[r]) for r in range(len(cores))]
+    assert slot == [4 * (r & 1) + (r >> 1) for r in range(len(cores))]
+    me, half = slot[rank], side[rank]
+    peers = [c for r, c in enumerate(cores) if side[r] == half and c != core]
+    mate = [c for c in cores if c != core and topo.chip(c) == topo.chip(core)][0]
+
+    eng = {"V": g.vector, "S": g.scalar, "P": g.tensor, "G": g, "Y": g.sync}
+    cnt, known, clk, wr, rd, bk, toks_all = {q: 0 for q in eng}, {q: {} for q in eng}, {}, {}, {}, {}, {}
+
+    def need(q, toks):
+        best = {}
+        for s, v in toks:
+            best[s] = max(best.get(s, 0), v)
+        todo = [(s, v) for s, v in best.items() if known[q].get(s, 0) < v]
+        todo = [t for t in todo if not any(o != t and clk[o].get(t[0], 0) >= t[1] for o in todo)]
+        for s, v in todo:
+            eng[q].wait_ge(T.sem[s], v)
+            for a, b in clk[(s, v)].items():
+                known[q][a] = max(known[q].get(a, 0), b)
+            known[q][s] = max(known[q].get(s, 0), v)
+
+    def pre(q, R, W, B=()):
+        toks = []
+        for r in R:
+            toks += wr.get(r, [])
+        for w in W:
+            toks += wr.get(w, []) + rd.get(w, [])
+        for b in B:
+            toks += [t for e, t in bk.get(b, {}).items() if e != q]
+        need(q, toks)
+
+    def post(q, tok, R, W, B=()):
+        clk[tok] = dict(known[q])
+        toks_all[tok[0]] = max(toks_all.get(tok[0], 0), tok[1])
+        for r in R:
+            rd[r] = [t for t in rd.get(r, []) if t[0] != tok[0]] + [tok]
+        for w in W:
+            wr[w], rd[w] = [tok], []
+        for b in B:
+            bk.setdefault(b, {})[q] = tok
+
+    def emit(q, calls, R=(), W=(), B=()):
+        pre(q, R, W, B)
+        for c in calls:
+            c().then_inc(T.sem["s" + q], 1)
+            cnt[q] += 1
+        post(q, ("s" + q, cnt[q]), R, W, B)
+
+    def dmas(q, pairs, sem, R=(), W=()):
+        pre(q, R, W)
+        for o, i in pairs:
+            eng[q].dma_start(out=o, in_=i).then_inc(T.sem[sem], 16)
+        post(q, (sem, 16 * len(pairs)), R, W)
+
+    def arrive(sem, val, W):
+        clk[(sem, val)] = {}
+        toks_all[sem] = val
+        for w in W:
+            wr[w] = wr.get(w, []) + [(sem, val)]
+
+    def ts(out, in0, s1, op0, s2=None, op1=None, R=(), W=(), B=()):
+        if op1 is None:
+            emit("V", [lambda: g.vector.tensor_scalar(out=out, in0=in0, scalar1=s1, scalar2=None, op0=op0)], R, W, B)
+        else:
+            emit("V", [lambda: g.vector.tensor_scalar(out=out, in0=in0, scalar1=s1, scalar2=s2, op0=op0, op1=op1)], R, W, B)
+
+    def tt(out, a, b, op, R=(), W=(), B=()):
+        emit("V", [lambda: g.vector.tensor_tensor(out=out, in0=a, in1=b, op=op)], R, W, B)
+
+    def cp(q, out, i, R=(), W=(), B=()):
+        if q == "V":
+            emit("V", [lambda: g.vector.tensor_copy(out=out, in_=i)], R, W, B)
+        else:
+            emit("S", [lambda: g.scalar.activation(out=out, in_=i, func=AF.Copy)], R, W, B)
+
+    def mms(groups, R=(), W=(), B=()):
+        emit("P", [(lambda m=m: g.tensor.matmul(out=m[0], lhsT=m[1], rhs=m[2], start=m[3], stop=m[4])) for m in groups], R, W, B)
+
+    def MB(n):
+        j = MATB.index(n)
+        return T.MBF[:, 128 * j:128 * j + 128]
+
+    def MX(n):
+        j = MATF.index(n)
+        return T.MFF[:, 128 * j:128 * j + 128]
+
+    def SL(n, q=None):
+        j = 144 * SLID.index(n)
+        return T.MSL[:, j:j + 144] if q is None else T.MSL[:, j + 15 - q:j + 143 - q]
+
+    dmas("Y", [(T.OI[:], T.opts[:])], "dOI", (), ["OI"])
+    pl = [(T.ST[32 * P:32 * P + 16, 128 * h:128 * h + 128], T.lw[32 * P + 16 * h:32 * P + 16 * h + 16, :]) for P in range(4) for h in (0, 1)]
+    pr = [(T.ST[32 * P + 16:32 * P + 32, 128 * h:128 * h + 128], T.rw[32 * P + 16 * h:32 * P + 16 * h + 16, :]) for P in range(4) for h in (0, 1)]
+    for o, i in pl:
+        g.sync.dma_start(out=o, in_=i).then_inc(T.sem.dST, 16)
+    for o, i in pr:
+        g.scalar.dma_start(out=o, in_=i).then_inc(T.sem.dST, 16)
+    arrive("dST", 16 * 16, ["ST"])
+
+    emit("G", [lambda: g.iota(T.CI[:, 0:1], [[0, 1]], 0, 1)], (), ["ci0"])
+    emit("G", [lambda: g.iota(T.XI[:], [[1, 144]], 0, 0, allow_small_or_imprecise_dtypes=True)], (), ["XI"])
+    emit("G", [lambda: g.iota(T.MI[:], [[1, 128]], 0, 0)], (), ["MI"])
+    emit("G", [lambda: g.iota(T.MKI[:], [[0, 9], [1, 8], [0, 16]], 0, 0)], (), ["MKI"])
+    ints = [("P", 5, 7), ("rho", 4, 1), ("grp", 4, 15), ("i", 0, 15), ("s", 0, 7), ("h3", 3, 1), ("blk", 3, 31), ("b0", 0, 1), ("b1", 1, 1)]
+    for j, (n, sh, m) in enumerate(ints):
+        ts(T.CI[:, j + 1:j + 2], T.CI[:, 0:1], sh, A.logical_shift_right, m, A.bitwise_and, ["ci0"], ["ci%d" % (j + 1)])
+    cp("V", T.CF[:, 0:10], T.CI[:, 0:10], ["ci%d" % j for j in range(10)], ["c_" + n for n in ["k"] + [x[0] for x in ints]])
+    names = ["k"] + [x[0] for x in ints]
+
+    def col(n):
+        j = names.index(n)
+        return T.CF[:, j:j + 1]
+
+    def lin(n, a, m, add):
+        names.append(n)
+        d = add if not isinstance(add, str) else col(add)
+        ts(col(n), col(a), float(m), A.mult, d, A.add, ["c_" + a] + (["c_" + add] if isinstance(add, str) else []), ["c_" + n])
+
+    lin("sgn", "rho", 2, -1.0)
+    lin("ntemp", "i", -1024, 0.0)
+    for b in (0, 1):
+        for h in (0, 1):
+            ts(T["LW%d" % b][:, 128 * me + 64 * h:128 * me + 64 * h + 64], T.ST[:, 128 * h + 64 * b:128 * h + 64 * b + 64], col("sgn"), A.mult,
+               col("ntemp"), A.add, ["ST", "c_sgn", "c_ntemp"], ["LW%do%d" % (b, h)])
+
+    def send(x, kind, buf, w):
+        blk = T[buf][:, w * me:w * me + w]
+        pre("G", [kind + x + "o0", kind + x + "o1"], [])
+        tag = buf[1] + x
+        m = topo.mask(core, peers[0])
+        ids = [DstId(rid=topo.addr(c)[0], pnc=topo.addr(c)[1]) for c in peers]
+        g.remote_dma_fused([RemoteDMATransfer(dst_ids=ids, dma_engine_mask=m, remote_sem=T.sem["p" + tag], srcs=[blk], dsts=[blk for c in peers])],
+                           local_sem=T.sem["l" + tag])
+        ne = len(topo.engines(core, peers[0]))
+        toks_all["l" + tag] = ne
+        arrive("p" + tag, len(peers) * ne, [kind + x + "p"])
+
+    def forward(x, kind, buf, w):
+        pre("G", [kind + x + "o0", kind + x + "o1", kind + x + "p"], [])
+        tag = buf[1] + x
+        blk = T[buf][:, 4 * w * half:4 * w * half + 4 * w]
+        rid, pid = topo.addr(mate)[0], topo.addr(mate)[1]
+        g.remote_dma(blk, blk, T.sem["m" + tag], T.sem["f" + tag], pid, rid, topo.mask(core, mate))
+        ne = len(topo.engines(core, mate))
+        toks_all["f" + tag] = ne
+        arrive("m" + tag, ne, [kind + x + "m"])
+
+    def have(kind, x, h):
+        return [kind + x + "o0", kind + x + "o1", kind + x + "p"] if h == half else [kind + x + "m"]
+
+    send("0", "LW", "LW0", 128)
+
+    def mat(dst, name, f, fr, h, w, wn=None):
+        ts(dst, f, col(h), A.is_equal, w if wn is None else col(wn), A.mult, [fr, "c_" + h] + ([] if wn is None else ["c_" + wn]), [name])
+
+    Xm = T.XI[:, 0:128]
+    flds = [("f8", 3, 31), ("f16", 4, 15), ("f31", 0, 31), ("f15", 0, 15), ("f119", 0, 119)]
+
+    def fld(n):
+        j = [x[0] for x in flds].index(n)
+        return T.MF[:, 128 * j:128 * j + 128]
+
+    fi = [(6, 255), (6, 1), (8, 3), (10, 1), (11, 3), (7, 1), (0, 63)]
+    for j, (sh, m) in enumerate(fi):
+        ts(T.FI[:, 128 * j:128 * j + 128], T.OI[:], sh, A.logical_shift_right, m, A.bitwise_and, ["OI"], ["FI%d" % j])
+    cp("V", T.FB[:], T.FI[:], ["FI%d" % j for j in range(7)], ["FB"])
+    ico = [1.0, 63.0, 12.0, -8.0, -30.0, -1.0]
+    for j in range(6):
+        mat(MB("ICO%d" % j), "ICO%d" % j, Xm, "XI", "k", ico[j])
+    mms([(T.K0[:, 0:128], MB("ICO%d" % j), T.FB[:, 128 * j:128 * j + 128], j == 0, j == 5) for j in range(6)],
+        ["FB"] + ["ICO%d" % j for j in range(6)], ["K0.h"], ["K0"])
+    lin("T32", "P", 32, 0.0)
+    lin("X0", "s", 1, "T32")
+    lin("OXn", "h3", 16, "X0")
+    lin("OXl", "OXn", 1, 8.0)
+    lin("n0", "rho", -1, 1.0)
+    lin("pa", "h3", -16, "X0")
+    lin("pb", "rho", 8, "pa")
+    lin("PERMh", "pb", 1, 16.0)
+    for h in (0, 1):
+        mat(MB("OXH%d" % h), "OXH%d" % h, Xm, "XI", "OXn", None, ["n0", "rho"][h])
+        mat(MB("OXL%d" % h), "OXL%d" % h, Xm, "XI", "OXl", None, ["n0", "rho"][h])
+    cp("V", T.HB[:], T.K0[:, 0:128], ["K0.h"], ["HB"], ["K0"])
+    lo = T.FB[:, 768:896]
+    for h, bank in ((0, "RV"), (1, "NP")):
+        mms([(T[bank][:, 0:128], MB("OXH%d" % h), T.HB[:], True, False), (T[bank][:, 0:128], MB("OXL%d" % h), lo, False, True)],
+            ["HB", "FB", "OXH%d" % h, "OXL%d" % h], [bank + ".x"], [bank])
+    mat(MB("PERM64"), "PERM64", Xm, "XI", "PERMh", 64.0)
+    mat(MB("PERM1"), "PERM1", Xm, "XI", "PERMh", 1.0)
+    for h, bank in ((0, "RV"), (1, "NP")):
+        for b in (0, 1):
+            c0 = 256 * me + 128 * b + 64 * h
+            cp("V" if h == 0 else "S", T.LOi[:, c0:c0 + 64], T[bank][:, 64 * b:64 * b + 64], [bank + ".x"], ["LOio%d" % h + ("b" if b else "")], [bank])
+    for h in (0, 1):
+        wr["LOio%d" % h] = wr["LOio%d" % h] + wr["LOio%db" % h]
+    send("i", "LO", "LOi", 256)
+    send("1", "LW", "LW1", 128)
+    forward("0", "LW", "LW0", 128)
+    forward("i", "LO", "LOi", 256)
+    forward("1", "LW", "LW1", 128)
+
+    mms([(T.K1[:, 0:128], MB("PERM64"), T.HB[:], True, False), (T.K1[:, 0:128], MB("PERM1"), lo, False, True)],
+        ["HB", "FB", "PERM64", "PERM1"], ["K1.o"], ["K1"])
+    cp("V", T.OF[:], T.K1[:, 0:128], ["K1.o"], ["OF0", "OF1"], ["K1"])
+    cp("V", T.OL[:], T.OF[:], ["OF0", "OF1"], ["OL0", "OL1"])
+
+    for j, (n, sh, m) in enumerate(flds):
+        ts(fld(n), T.MI[:], sh, A.logical_shift_right, m, A.bitwise_and, ["MI"], [n])
+    for p in range(4):
+        lin("kr%d" % p, "k", 1, -32.0 * p)
+        mat(MB("REP%d" % p), "REP%d" % p, fld("f31"), "f31", "kr%d" % p, 1.0)
+        if p >= 4 - NREP:
+            mat(MX("REPF%d" % p), "REPF%d" % p, fld("f31"), "f31", "kr%d" % p, 1.0)
+    emit("V", [lambda: g.vector.memset(T.W[:, 8192:8200], -BIG)], (), ["Wz"])
+    lin("sent", "h3", -128, 128.0)
+    emit("V", [lambda: g.vector.memset(MB("ONES"), 1.0)], (), ["ONES"])
+    ts(T.OT[:, 8192:8208], T.MBF[:, 128 * MATB.index("ONES"):128 * MATB.index("ONES") + 16], col("sent"), A.mult, None, None, ["ONES", "c_sent"], ["OTz"])
+    ts(T.MK[:], T.MKI[:], col("s"), A.is_equal, None, None, ["MKI", "c_s"], ["MK"])
+    lin("own15", "grp", 16, 15.0)
+    lin("ot", "rho", -32, "own15")
+    lin("oth15", "ot", 1, 16.0)
+    lin("w64", "h3", -63, 64.0)
+    Xs = T.XI[:]
+    mat(SL("BKO"), "BKO", Xs, "XI", "own15", None, "w64")
+    mat(SL("BKX"), "BKX", Xs, "XI", "oth15", None, "w64")
+
+    def late():
+        mat(SL("OWN"), "OWN", Xs, "XI", "own15", 1.0)
+        mat(SL("OTH"), "OTH", Xs, "XI", "oth15", 1.0)
+        for j, d in enumerate(DELTA):
+            lin("d%d" % j, "own15", 1, float(d))
+            mat(SL("BD%d" % j), "BD%d" % j, Xs, "XI", "d%d" % j, -1.0)
+        ts(T.MX[:, 0:144], SL("OWN"), 32.0, A.mult, None, None, ["OWN"], ["MX0"])
+        for j in range(6):
+            tt(SL("BD%d" % j), SL("BD%d" % j), T.MX[:, 0:144], A.add, ["MX0"], ["BD%d" % j])
+        lin("thr1", "b0", 1, -0.5)
+        lin("thr2", "b1", 1, -0.5)
+        mat(MB("IB"), "IB", Xm, "XI", "k", 1.0)
+        mat(MB("E8"), "E8", fld("f8"), "f8", "blk", -2.0)
+        ts(MB("GT"), Xm, col("k"), A.is_gt, None, None, ["XI", "c_k"], ["GT"])
+        tt(MB("E8"), MB("E8"), MB("GT"), A.mult, ["GT"], ["E8"])
+        tt(MB("YM"), MB("E8"), MB("IB"), A.add, ["E8", "IB"], ["YM"])
+        lin("bf", "rho", -4, "blk")
+        lin("blkf", "bf", 1, 2.0)
+        mat(MX("CH"), "CH", fld("f8"), "f8", "blkf", 1.0)
+        lin("ta", "rho", -16, "X0")
+        lin("T0", "ta", 1, 16.0)
+        lin("T8", "ta", 1, 24.0)
+        mat(MB("ENT0"), "ENT0", Xm, "XI", "T0", None, "w64")
+        mat(MB("ENT1"), "ENT1", Xm, "XI", "T8", None, "w64")
+        mat(MB("KEEPN"), "KEEPN", Xm, "XI", "k", -16384.0)
+        lin("g0", "h3", -1, 1.0)
+        for h, gn in ((0, "g0"), (1, "h3")):
+            lin("a%d" % h, gn, -BIG, 0.0)
+            lin("q%d" % h, gn, -256, 0.0)
+            mat(MB("ANY%d" % h), "ANY%d" % h, fld("f16"), "f16", "grp", None, "a%d" % h)
+            mat(MB("KX%d" % h), "KX%d" % h, fld("f119"), "f119", "T0", None, gn)
+            mat(MB("KN%d" % h), "KN%d" % h, fld("f119"), "f119", "T0", None, "q%d" % h)
+        lin("sa", "rho", -32, "k")
+        lin("SWh", "sa", 1, 16.0)
+        mat(MX("SW"), "SW", Xm, "XI", "SWh", 1.0)
+        mat(MX("NSW"), "NSW", Xm, "XI", "SWh", -1.0)
+        mat(MX("IF"), "IF", Xm, "XI", "k", 1.0)
+        tt(MX("ISW"), MX("SW"), MX("IF"), A.add, ["SW", "IF"], ["ISW"])
+        lin("temp", "i", 1024, 0.0)
+        names.append("kz")
+        ts(col("kz"), col("k"), 0.0, A.is_equal, -1024.0, A.mult, ["c_k"], ["c_kz"])
+        lin("kp", "kz", -1, 0.0)
+        ts(MB("TMN"), fld("f15"), col("kz"), A.mult, None, None, ["f15", "c_kz"], ["TMN"])
+        ts(MB("TMP"), fld("f15"), col("kp"), A.mult, None, None, ["f15", "c_kp"], ["TMP"])
+        emit("V", [lambda: g.vector.memset(T.RS[:], 0.0)], (), ["RS"])
+        emit("V", [lambda: g.vector.memset(T.RS[:, 0::8], -BIG)], (), ["RS"])
+        lin("iv", "rho", -8, "OXn")
+        lin("INVh", "iv", 1, 8.0)
+        mat(MX("INVF"), "INVF", Xm, "XI", "INVh", 1.0)
+        for j, c in enumerate([-4032.0, -768.0, 512.0, 1920.0, 64.0]):
+            mat(MB("INV%d" % j), "INV%d" % j, Xm, "XI", "INVh", c)
+
+    OTALL = ["OTz"] + ["OT%d%d%d" % (b, p, h) for b in (0, 1) for p in range(4) for h in (0, 1)]
+    WALL = ["Wz"] + ["W%d%d%d" % (b, p, h) for b in (0, 1) for p in range(4) for h in (0, 1)]
+    rb = [("UP", 0, "UPa"), ("UP", 512, "UPb"), ("YY", 0, "YY"), ("DD", 0, "DD")]
+    nb = [0]
+
+    def rep_o(x, b, h, qs):
+        for p in range(4):
+            buf, c0, bank = rb[nb[0] % 4]
+            nb[0] += 1
+            out = T[buf][:, c0:c0 + 512]
+            if x == "i":
+                ms = [(T[buf][:, c0 + 128 * j:c0 + 128 * j + 128], MB("REP%d" % p),
+                       T.LOi[:, 256 * (4 * h + j) + 128 * b:256 * (4 * h + j) + 128 * b + 128], True, True) for j in range(4)]
+            else:
+                ms = [(out, MB("REP%d" % p), T["LO" + x][:, 512 * h:512 * h + 512], True, True)]
+            mms(ms, have("LO", x, h) + ["REP%d" % p], [bank + ".r"], [bank])
+            d0 = 4096 * b + 1024 * p + 512 * h
+            cp(qs[p % len(qs)], T.OT[:, d0:d0 + 512], out, [bank + ".r"], ["OT%d%d%d" % (b, p, h)], [bank])
+
+    def rep_w_dma(x, b, h):
+        n = 4 - NREP
+        dmas("Y", [(T.W[32 * pp:32 * pp + 32, 4096 * b + 1024 * p + 512 * h:4096 * b + 1024 * p + 512 * h + 512],
+                    T["LW" + x][32 * p:32 * p + 32, 512 * h:512 * h + 512]) for p in range(n) for pp in range(4)],
+             "dW%s%d" % (x, h), have("LW", x, h), ["W%d%d%d" % (b, p, h) for p in range(n)])
+
+    def rep_w_pe(x, b, h, q):
+        for p in range(4 - NREP, 4):
+            buf, c0, bank = rb[nb[0] % 4]
+            nb[0] += 1
+            out = T[buf][:, c0:c0 + 512]
+            mms([(out, MX("REPF%d" % p), T["LW" + x][:, 512 * h:512 * h + 512], True, True)], have("LW", x, h) + ["REPF%d" % p], [bank + ".r"], [bank])
+            d0 = 4096 * b + 1024 * p + 512 * h
+            cp(q, T.W[:, d0:d0 + 512], out, [bank + ".r"], ["W%d%d%d" % (b, p, h)], [bank])
+
+    def expand(x, b):
+        for q in range(16):
+            hh = q >> 3
+            cp("S", T["XE%d" % b][:, q::16], T["LW" + x][:, 128 * me + 64 * hh:128 * me + 64 * hh + 64], ["LW%so%d" % (x, hh)], ["XE%d.%d" % (b, q)])
+
+    def lists_gather(t):
+        b = t & 1
+        tt(T.GM[:], T.OT[:].indirect(T.OL[:, 64 * b:64 * b + 64]), T.MK[:, 16 * t:16 * t + 1024], A.mult, OTALL + ["OL%d" % b, "MK"], ["GM"])
+
+    def lists(t):
+        b = t & 1
+        for n, bank in (("BKO", "K0"), ("BKX", "K1")):
+            mms([(T[bank][:, 0:64], SL(n, q), T.GM[:, q::16], q == 0, q == 15) for q in range(16)], ["GM", n], [bank + ".k"], [bank])
+        cp("V", T.KL[:, 0:64], T.K0[:, 0:64], ["K0.k"], ["KL0"], ["K0"])
+        ts(T.KC[:], T.K0[:, 0:64], -8192.0, A.add, None, None, ["K0.k"], ["KC"], ["K0"])
+        ts(T.HAS[:], T.OF[:, 64 * b:64 * b + 64], 8191.5, A.is_lt, None, None, ["OF%d" % b], ["HAS"])
+        cp("V", T.KL[:, 64:128], T.K1[:, 0:64], ["K1.k"], ["KL1"], ["K1"])
+
+    def natural(b):
+        o = T.OF[:, 64 * b:64 * b + 64]
+        cp("V", T.YI[:], o, ["OF%d" % b], ["YI"])
+        for j, (sh, m) in enumerate([(12, 1), (10, 3), (9, 1), (7, 3), (6, 1)]):
+            ts(T.YFI[:, 64 * j:64 * j + 64], T.YI[:], sh, A.logical_shift_right, m, A.bitwise_and, ["YI"], ["YFI%d" % j])
+        cp("V", T.YFB[:], T.YFI[:], ["YFI%d" % j for j in range(5)], ["YFB"])
+        mms([(T.YY[:, 128:192], MX("INVF"), o, True, False)]
+            + [(T.YY[:, 128:192], MB("INV%d" % j), T.YFB[:, 64 * j:64 * j + 64], False, j == 4) for j in range(5)],
+            ["OF%d" % b, "YFB", "INVF"] + ["INV%d" % j for j in range(5)], ["YY.n"], ["YY"])
+        cp("S", T["YO%d" % b][:], T.YY[:, 128:192], ["YY.n"], ["YO%d" % b], ["YY"])
+        dmas("Y", [(T.yo[:, 64 * b:64 * b + 64], T["YO%d" % b][:])], "dO%d" % b, ["YO%d" % b], [])
+
+    def round_(t):
+        b, m = t & 1, 1 + t
+        x = {0: "0", 1: "1", 2: "2"}[t]
+        nx = {0: "2", 1: "3", 2: None}[t]
+        xe = ["XE%d.%d" % (b, q) for q in range(16)]
+        Wt = T.W[:]
+        mine = "LW%so" % x
+        ol = T.OL[:, 64 * b:64 * b + 64]
+        emit("S", [lambda: g.scalar.activation(out=T.U[:], in_=Wt.indirect(ol), func=AF.Copy)], WALL + ["OL%d" % b], ["U"])
+        cp("S", T.UP[:], T.U[:], ["U"], ["UPa.r", "UPb.r"], ["UPa", "UPb"])
+        XE = T["XE%d" % b]
+        tt(T.VO[:], Wt.indirect(T.KL[:, 0:64]), XE[:], A.is_gt, WALL + ["KL0"] + xe, ["VO"])
+        mms([(T.RV[:, 0:64], SL("OWN", q), T.VO[:, q::16], q == 0, False) for q in range(16)], ["VO", "OWN"], ["RV.v"], ["RV"])
+        tt(T.VX[:], Wt.indirect(T.KL[:, 64:128]), XE[:], A.is_lt, WALL + ["KL1"] + xe, ["VX"])
+        mms([(T.RV[:, 0:64], SL("OTH", q), T.VX[:, q::16], False, q == 15) for q in range(16)], ["VX", "OTH"], ["RV.v2"], ["RV"])
+        st = {1: [(0, 1, 2)], 2: [(0, 2, 4), (1, 3, 4)], 3: [(0, 3, 4), (1, 2, 4)]}[m]
+        for u, v, s in st:
+            for y, z in ((u, v), (v, u)):
+                tt(T.C[:, y::s], T.U[:, y::s], T.UP[:, z::s], A.is_gt, ["U", "UPa.r", "UPb.r"], ["C%d" % y], ["UPa", "UPb"])
+        cs = ["C%d" % y for u, v, s in st for y in (u, v)]
+        thr = "thr1" if m == 1 else "thr2"
+        mms([(T.DD[:, 0:64], SL("BD%d" % DELTA.index((q ^ m) - q), q), T.C[:, q::16], q == 0, q == 15) for q in range(16)],
+            cs + ["BD%d" % j for j in range(6)], ["DD.d"], ["DD"])
+        ts(T.R1[:], T.RV[:, 0:64], 1024.0, A.mult, col(thr), A.add, ["RV.v", "RV.v2", "c_" + thr], ["R1"], ["RV"])
+        tt(T.REV[:], T.DD[:, 0:64], T.R1[:], A.is_ge, ["DD.d", "R1"], ["REV"], ["DD"])
+        mms([(T.YY[:, 0:64], MB("YM"), T.REV[:], True, True)], ["REV", "YM"], ["YY.y"], ["YY"])
+        ts(T.ND[:], T.DD[:, 0:64], col(thr), A.is_ge, None, None, ["DD.d", "c_" + thr], ["ND"], ["DD"])
+        tt(T.NH[:], T.ND[:], T.HAS[:], A.mult, ["ND", "HAS"], ["NH"])
+        ts(T.FF[:], T.YY[:, 0:64], 0.5, A.is_gt, None, None, ["YY.y"], ["FF"], ["YY"])
+        tt(T.FK[:], T.FF[:], T.KC[:], A.mult, ["FF", "KC"], ["FK"])
+        mms([(T.YY[:, 64:128], MX("CH"), T.FK[:], True, True)], ["FK", "CH"], ["YY.c"], ["YY"])
+        tt(T.KEEP[:], T.NH[:], T.FF[:], A.subtract, ["NH", "FF"], ["KEEP"])
+        tt(T.OK[:], T.OF[:, 64 * b:64 * b + 64], T.KEEP[:], A.mult, ["OF%d" % b, "KEEP"], ["OK"])
+        mms([(T.NP[:, 0:64], MB("KEEPN"), T.KEEP[:], True, False)], ["KEEP", "KEEPN"], ["NP.n"], ["NP"])
+        ts(T.CL[:], T.YY[:, 64:128], 8192.0, A.add, None, None, ["YY.c"], ["CL"], ["YY"])
+        if nx:
+            mms([(T.RV[:, 64 * h + 128:64 * h + 192], MB("KX%d" % h), T.KEEP[:], True, True) for h in (0, 1)], ["KEEP", "KX0", "KX1"], ["RV.k"], ["RV"])
+        emit("V", [lambda: g.vector.tensor_copy(out=T.E[:, 0:512], in_=T.OT[:].indirect(T.CL[:, 0:32]))], OTALL + ["CL"], ["E0"])
+        emit("S", [lambda: g.scalar.activation(out=T.E[:, 512:1024], in_=T.OT[:].indirect(T.CL[:, 32:64]), func=AF.Copy)], OTALL + ["CL"], ["E1"])
+        mms([(T.NP[:, 0:64], MB("ENT0"), T.E[:, 0::16], False, False), (T.NP[:, 0:64], MB("ENT1"), T.E[:, 8::16], False, True)],
+            ["E0", "E1", "ENT0", "ENT1"], ["NP.n2"], ["NP"])
+        n = T.OF[:, 64 * b:64 * b + 64]
+        tt(n, T.NP[:, 0:64], T.OK[:], A.max, ["NP.n", "NP.n2", "OK"], ["OF%d" % b], ["NP"])
+        cp("V", ol, n, ["OF%d" % b], ["OL%d" % b])
+        for h, bank in ((0, "K0"), (1, "K1")):
+            mms([(T[bank][:, 0:64], MX("NSW"), T["LW" + x][:, 128 * me + 64 * h:128 * me + 64 * h + 64], True, False),
+                 (T[bank][:, 0:64], MB("TMN"), MB("ONES")[:, 0:64] if False else T.MBF[:, 128 * MATB.index("ONES"):128 * MATB.index("ONES") + 64], False, False)],
+                [mine + "0", mine + "1", "NSW", "TMN", "ONES"], [bank + ".a"], [bank])
+        emit("S", [lambda: g.scalar.activation(out=T.U5[:, 512:1024], in_=Wt.indirect(T.OL[:, 64 * b + 32:64 * b + 64]), func=AF.Copy)],
+             WALL + ["OL%d" % b], ["U51"])
+        emit("V", [lambda: g.vector.tensor_copy(out=T.U5[:, 0:512], in_=Wt.indirect(T.OL[:, 64 * b:64 * b + 32]))], WALL + ["OL%d" % b], ["U50"])
+        ts(T.HN[:], n, 8191.5, A.is_lt, None, None, ["OF%d" % b], ["HN"])
+        if nx:
+            old = T.LOi[:, 256 * me + 128 * b:256 * me + 128 * b + 128]
+            for h in (0, 1):
+                mms([(T.DD[:, 128 + 64 * h:192 + 64 * h], MB("KN%d" % h), T.KEEP[:], True, False),
+                     (T.DD[:, 128 + 64 * h:192 + 64 * h], MB("IB"), T.E[:, 8 * h::16], False, True)],
+                    ["KEEP", "E0", "E1", "IB", "KN%d" % h], ["DD.x%d" % h], ["DD"])
+            tt(T.OXA[:], T.RV[:, 128:256], old, A.mult, ["RV.k", "LOio0", "LOio1"], ["OXA"], ["RV"])
+        for h, bank in ((0, "K0"), (1, "K1")):
+            mms([(T[bank][:, 0:64], MB("ANY%d" % h), T.HN[:], False, True)], ["HN", "ANY%d" % h], [bank + ".b"], [bank])
+        if nx:
+            for h in (0, 1):
+                tt(T["LO" + nx][:, 128 * me + 64 * h:128 * me + 64 * h + 64], T.DD[:, 128 + 64 * h:192 + 64 * h], T.OXA[:, 64 * h:64 * h + 64], A.max,
+                   ["DD.x%d" % h, "OXA"], ["LO%so%d" % (nx, h)], ["DD"])
+            send(nx, "LO", "LO" + nx, 128)
+        for h in (0, 1):
+            emit("V", [lambda: g.vector.tensor_tensor_scan(out=T.MX[:, 512 * h:512 * h + 512], data0=T.RS[:], data1=T.U5[:, 512 * h:512 * h + 512],
+                                                           initial=-2.0 * BIG, op0=A.add, op1=A.max)], ["RS", "U5%d" % h], ["MX%d" % h])
+        for h, bank in ((0, "K0"), (1, "K1")):
+            tt(T.OWNW[:, 64 * h:64 * h + 64], T.MX[:, 7 + 8 * h::16], T[bank][:, 0:64], A.max, ["MX0", "MX1", bank + ".a", bank + ".b"], ["OWN%d" % h], [bank])
+        mms([(T.NP[:, 256:384], MB("TMP"), MB("ONES"), True, False)], ["TMP", "ONES"], ["NP.t"], ["NP"])
+        mms([(T.RV[:, 256:384], MX("ISW"), T.OWNW[:], True, True)], ["OWN0", "OWN1", "ISW"], ["RV.s"], ["RV"])
+        mms([(T.NP[:, 256:384], MX("SW"), T.OWNW[:], False, True)], ["OWN0", "OWN1", "SW"], ["NP.t2"], ["NP"])
+        ts(T.M1[:], T.RV[:, 256:384], 0.0, A.min, col("n0"), A.add, ["RV.s", "c_n0"], ["M1"], ["RV"])
+        ts(T.M2[:], T.M1[:], 1, A.arith_shift_right, None, None, ["M1"], ["M2"])
+        if nx:
+            tt(T["LW" + nx][:, 128 * me:128 * me + 128], T.M2[:], T.NP[:, 256:384], A.subtract, ["M2", "NP.t", "NP.t2"], ["LW%so0" % nx, "LW%so1" % nx], ["NP"])
+            send(nx, "LW", "LW" + nx, 128)
+            forward(nx, "LO", "LO" + nx, 128)
+            forward(nx, "LW", "LW" + nx, 128)
+            src, sr = T["LW" + nx][:, 128 * me:128 * me + 128], ["LW%so0" % nx, "LW%so1" % nx]
+        else:
+            tt(T.NF[:], T.M2[:], T.NP[:, 256:384], A.subtract, ["M2", "NP.t", "NP.t2"], ["NF"], ["NP"])
+            src, sr = T.NF[:], ["NF"]
+        if t > 0:
+            ts(T["YW%d" % b][:], src, col("temp"), A.add, col("sgn"), A.mult, sr + ["c_temp", "c_sgn"], ["YW%d" % b])
+            outs = [[], []]
+            for P in range(4):
+                for h in (0, 1):
+                    r0 = 32 * P + 16 * h
+                    outs[0].append((T.yl[r0:r0 + 16, 64 * b:64 * b + 64], T["YW%d" % b][32 * P:32 * P + 16, 64 * h:64 * h + 64]))
+                    outs[1].append((T.yr[r0:r0 + 16, 64 * b:64 * b + 64], T["YW%d" % b][32 * P + 16:32 * P + 32, 64 * h:64 * h + 64]))
+            for q, o in (("Y", outs[0]), ("S", outs[1])):
+                pre(q, ["YW%d" % b], [])
+                for d, s in o:
+                    eng[q].dma_start(out=d, in_=s).then_inc(T.sem["dY%d" % b], 16)
+            toks_all["dY%d" % b] = 16 * 16
+            natural(b)
+
+    hs = [half, 1 - half]
+    expand("0", 0)
+    for h in hs:
+        rep_w_dma("0", 0, h)
+    for b in (0, 1):
+        rep_o("i", b, hs[0], "VS")
+    for h in hs:
+        rep_w_pe("0", 0, h, "S")
+    late()
+    for b in (0, 1):
+        rep_o("i", b, hs[1], "VS")
+    for h in hs:
+        rep_w_dma("1", 1, h)
+    lists_gather(0)
+    lists(0)
+    for h in hs:
+        rep_w_pe("1", 1, h, "S")
+    round_(0)
+    expand("1", 1)
+    for t, x, b in ((1, "2", 0), (2, "3", 1)):
+        for h in hs:
+            rep_w_dma(x, b, h)
+        for h in hs:
+            rep_o(x, b, h, "VS")
+        lists_gather(t)
+        rep_w_pe(x, b, hs[0], "S")
+        lists(t)
+        rep_w_pe(x, b, hs[1], "S")
+        if t == 1:
+            pass
+        round_(t)
+        if t == 1:
+            expand("2", 0)
+    for s in SEMAPHORES:
+        if toks_all.get(s, 0) > known["G"].get(s, 0):
+            g.wait_ge(T.sem[s], toks_all[s])

@@ -3,19 +3,20 @@ from concourse.mybir import AluOpType as A, ActivationFunctionType as AF
 
 EXW = ["0", "1", "2", "3"]
 EXO = ["i", "2", "3"]
-NREP = 1
+NREP = {"0": (2, 2), "1": (1, 1), "2": (1, 2), "3": (1, 2)}
+FREE = ["LW0", "LOi", "LW1", "LO2", "LO3"]
 BIG = 2.0 ** 23
 MATB = (["REP%d" % p for p in range(4)] + ["YM", "E8", "GT", "ENT0", "ENT1", "KEEPN", "ANY0", "ANY1", "KX0", "KX1", "KN0", "KN1", "IB",
         "TMN", "TMP", "ONES", "PERM64", "PERM1", "OXH0", "OXH1", "OXL0", "OXL1"]
         + ["ICO%d" % f for f in range(6)] + ["INV%d" % f for f in range(5)])
-MATF = ["REPF%d" % p for p in range(4)] + ["CH", "SW", "NSW", "ISW", "INVF", "IF"]
-SLID = ["OWN", "OTH", "BKO", "BKX"] + ["BD%d" % d for d in range(6)]
+MATF = ["REPF%d" % p for p in range(4)] + ["CH", "SW", "NSW", "ISW", "INVF"]
+SLID = ["OTH", "BKO", "BKX"] + ["BD%d" % d for d in range(6)]
 DELTA = [1, -1, 2, -2, 3, -3]
 
 SCRATCH = {
     "W": ("sbuf", [128, 8200], "float32"), "OT": ("sbuf", [128, 8208], "bfloat16"),
     "MBF": ("sbuf", [128, 128 * len(MATB)], "bfloat16"), "MFF": ("sbuf", [128, 128 * len(MATF)], "float32"),
-    "MSL": ("sbuf", [128, 144 * len(SLID)], "bfloat16"),
+    "MSL": ("sbuf", [128, 144 * len(SLID) + 160], "bfloat16"),
     "CI": ("sbuf", [128, 16], "int32"), "CF": ("sbuf", [128, 64], "float32"),
     "XI": ("sbuf", [128, 144], "float32"), "MI": ("sbuf", [128, 128], "int32"), "MF": ("sbuf", [128, 640], "int32"),
     "MKI": ("sbuf", [128, 1152], "int32"), "MK": ("sbuf", [128, 1152], "bfloat16"), "RS": ("sbuf", [128, 512], "float32"),
@@ -129,6 +130,9 @@ def rank_program(g, core, T, topo):
         else:
             emit("S", [lambda: g.scalar.activation(out=out, in_=i, func=AF.Copy)], R, W, B)
 
+    def sc(dst, src, scale, R, W):
+        emit("S", [lambda: g.scalar.activation(out=dst, in_=src, func=AF.Copy, scale=float(scale))], R, W)
+
     def mms(groups, R=(), W=(), B=()):
         emit("P", [(lambda m=m: g.tensor.matmul(out=m[0], lhsT=m[1], rhs=m[2], start=m[3], stop=m[4])) for m in groups], R, W, B)
 
@@ -141,16 +145,15 @@ def rank_program(g, core, T, topo):
         return T.MFF[:, 128 * j:128 * j + 128]
 
     def SL(n, q=None):
-        j = 144 * SLID.index(n)
+        j = 4 if n == "OWN" else 160 + 144 * SLID.index(n)
         return T.MSL[:, j:j + 144] if q is None else T.MSL[:, j + 15 - q:j + 143 - q]
 
     dmas("Y", [(T.OI[:], T.opts[:])], "dOI", (), ["OI"])
-    pl = [(T.ST[32 * P:32 * P + 16, 128 * h:128 * h + 128], T.lw[32 * P + 16 * h:32 * P + 16 * h + 16, :]) for P in range(4) for h in (0, 1)]
-    pr = [(T.ST[32 * P + 16:32 * P + 32, 128 * h:128 * h + 128], T.rw[32 * P + 16 * h:32 * P + 16 * h + 16, :]) for P in range(4) for h in (0, 1)]
-    for o, i in pl:
-        g.sync.dma_start(out=o, in_=i).then_inc(T.sem.dST, 16)
-    for o, i in pr:
-        g.scalar.dma_start(out=o, in_=i).then_inc(T.sem.dST, 16)
+    for q, r0, src in (("Y", 0, T.lw), ("S", 16, T.rw)):
+        for P in range(4):
+            for h in (0, 1):
+                eng[q].dma_start(out=T.ST[32 * P + r0:32 * P + r0 + 16, 128 * h:128 * h + 128],
+                                 in_=src[32 * P + 16 * h:32 * P + 16 * h + 16, :]).then_inc(T.sem.dST, 16)
     arrive("dST", 16 * 16, ["ST"])
 
     emit("G", [lambda: g.iota(T.CI[:, 0:1], [[0, 1]], 0, 1)], (), ["ci0"])
@@ -160,20 +163,43 @@ def rank_program(g, core, T, topo):
     ints = [("P", 5, 7), ("rho", 4, 1), ("grp", 4, 15), ("i", 0, 15), ("s", 0, 7), ("h3", 3, 1), ("blk", 3, 31), ("b0", 0, 1), ("b1", 1, 1)]
     for j, (n, sh, m) in enumerate(ints):
         ts(T.CI[:, j + 1:j + 2], T.CI[:, 0:1], sh, A.logical_shift_right, m, A.bitwise_and, ["ci0"], ["ci%d" % (j + 1)])
-    cp("V", T.CF[:, 0:10], T.CI[:, 0:10], ["ci%d" % j for j in range(10)], ["c_" + n for n in ["k"] + [x[0] for x in ints]])
     names = ["k"] + [x[0] for x in ints]
+    cp("V", T.CF[:, 0:10], T.CI[:, 0:10], ["ci%d" % j for j in range(10)], ["c_" + n for n in names])
 
     def col(n):
         j = names.index(n)
         return T.CF[:, j:j + 1]
 
-    def lin(n, a, m, add):
+    def lin(n, a, m, add, q="S"):
         names.append(n)
         d = add if not isinstance(add, str) else col(add)
-        ts(col(n), col(a), float(m), A.mult, d, A.add, ["c_" + a] + (["c_" + add] if isinstance(add, str) else []), ["c_" + n])
+        R = ["c_" + a] + (["c_" + add] if isinstance(add, str) else [])
+        if q == "S":
+            emit("S", [lambda: g.scalar.activation(out=col(n), in_=col(a), func=AF.Identity, bias=d, scale=float(m))], R, ["c_" + n])
+        else:
+            ts(col(n), col(a), float(m), A.mult, d, A.add, R, ["c_" + n])
 
-    lin("sgn", "rho", 2, -1.0)
-    lin("ntemp", "i", -1024, 0.0)
+    def mat(dst, name, f, fr, h, w, wn=None):
+        ts(dst, f, col(h), A.is_equal, w if wn is None else col(wn), A.mult, [fr, "c_" + h] + ([] if wn is None else ["c_" + wn]), [name])
+
+    Xm, Xs = T.XI[:, 0:128], T.XI[:]
+    lin("sgn", "rho", 2, -1.0, "V")
+    lin("ntemp", "i", -1024, 0.0, "V")
+    ico = [1.0, 63.0, 12.0, -8.0, -30.0, -1.0]
+    mat(MB("IB"), "IB", Xm, "XI", "k", 1.0)
+    for j in range(1, 6):
+        sc(MB("ICO%d" % j), MB("IB"), ico[j], ["IB"], ["ICO%d" % j])
+    lin("X0", "P", 32, "s", "V")
+    lin("OXn", "h3", 16, "X0", "V")
+    lin("n0", "rho", -1, 1.0, "V")
+    for h in (0, 1):
+        mat(MB("OXH%d" % h), "OXH%d" % h, Xm, "XI", "OXn", None, ["n0", "rho"][h])
+    lin("OXl", "OXn", 1, 8.0, "V")
+    for h in (0, 1):
+        mat(MB("OXL%d" % h), "OXL%d" % h, Xm, "XI", "OXl", None, ["n0", "rho"][h])
+    fi = [(6, 255), (6, 1), (8, 3), (10, 1), (11, 3), (7, 1), (0, 63)]
+    for j, (sh, m) in enumerate(fi):
+        ts(T.FI[:, 128 * j:128 * j + 128], T.OI[:], sh, A.logical_shift_right, m, A.bitwise_and, ["OI"], ["FI%d" % j])
     for b in (0, 1):
         for h in (0, 1):
             ts(T["LW%d" % b][:, 128 * me + 64 * h:128 * me + 64 * h + 64], T.ST[:, 128 * h + 64 * b:128 * h + 64 * b + 64], col("sgn"), A.mult,
@@ -183,10 +209,9 @@ def rank_program(g, core, T, topo):
         blk = T[buf][:, w * me:w * me + w]
         pre("G", [kind + x + "o0", kind + x + "o1"], [])
         tag = buf[1] + x
-        m = topo.mask(core, peers[0])
         ids = [DstId(rid=topo.addr(c)[0], pnc=topo.addr(c)[1]) for c in peers]
-        g.remote_dma_fused([RemoteDMATransfer(dst_ids=ids, dma_engine_mask=m, remote_sem=T.sem["p" + tag], srcs=[blk], dsts=[blk for c in peers])],
-                           local_sem=T.sem["l" + tag])
+        g.remote_dma_fused([RemoteDMATransfer(dst_ids=ids, dma_engine_mask=topo.mask(core, peers[0]), remote_sem=T.sem["p" + tag], srcs=[blk],
+                                              dsts=[blk for c in peers])], local_sem=T.sem["l" + tag])
         ne = len(topo.engines(core, peers[0]))
         toks_all["l" + tag] = ne
         arrive("p" + tag, len(peers) * ne, [kind + x + "p"])
@@ -196,53 +221,32 @@ def rank_program(g, core, T, topo):
         tag = buf[1] + x
         blk = T[buf][:, 4 * w * half:4 * w * half + 4 * w]
         rid, pid = topo.addr(mate)[0], topo.addr(mate)[1]
-        g.remote_dma(blk, blk, T.sem["m" + tag], T.sem["f" + tag], pid, rid, topo.mask(core, mate))
-        ne = len(topo.engines(core, mate))
-        toks_all["f" + tag] = ne
-        arrive("m" + tag, ne, [kind + x + "m"])
+        es = topo.engines(core, mate)
+        if kind + x in FREE:
+            es = [e for e in es if e not in topo.engines(core, peers[0])]
+        g.remote_dma(blk, blk, T.sem["m" + tag], T.sem["f" + tag], pid, rid, sum(1 << e for e in es))
+        toks_all["f" + tag] = len(es)
+        arrive("m" + tag, len(es), [kind + x + "m"])
 
     def have(kind, x, h):
         return [kind + x + "o0", kind + x + "o1", kind + x + "p"] if h == half else [kind + x + "m"]
 
     send("0", "LW", "LW0", 128)
 
-    def mat(dst, name, f, fr, h, w, wn=None):
-        ts(dst, f, col(h), A.is_equal, w if wn is None else col(wn), A.mult, [fr, "c_" + h] + ([] if wn is None else ["c_" + wn]), [name])
-
-    Xm = T.XI[:, 0:128]
     flds = [("f8", 3, 31), ("f16", 4, 15), ("f31", 0, 31), ("f15", 0, 15), ("f119", 0, 119)]
 
     def fld(n):
         j = [x[0] for x in flds].index(n)
         return T.MF[:, 128 * j:128 * j + 128]
 
-    fi = [(6, 255), (6, 1), (8, 3), (10, 1), (11, 3), (7, 1), (0, 63)]
-    for j, (sh, m) in enumerate(fi):
-        ts(T.FI[:, 128 * j:128 * j + 128], T.OI[:], sh, A.logical_shift_right, m, A.bitwise_and, ["OI"], ["FI%d" % j])
     cp("V", T.FB[:], T.FI[:], ["FI%d" % j for j in range(7)], ["FB"])
-    ico = [1.0, 63.0, 12.0, -8.0, -30.0, -1.0]
-    for j in range(6):
-        mat(MB("ICO%d" % j), "ICO%d" % j, Xm, "XI", "k", ico[j])
-    mms([(T.K0[:, 0:128], MB("ICO%d" % j), T.FB[:, 128 * j:128 * j + 128], j == 0, j == 5) for j in range(6)],
-        ["FB"] + ["ICO%d" % j for j in range(6)], ["K0.h"], ["K0"])
-    lin("T32", "P", 32, 0.0)
-    lin("X0", "s", 1, "T32")
-    lin("OXn", "h3", 16, "X0")
-    lin("OXl", "OXn", 1, 8.0)
-    lin("n0", "rho", -1, 1.0)
-    lin("pa", "h3", -16, "X0")
-    lin("pb", "rho", 8, "pa")
-    lin("PERMh", "pb", 1, 16.0)
-    for h in (0, 1):
-        mat(MB("OXH%d" % h), "OXH%d" % h, Xm, "XI", "OXn", None, ["n0", "rho"][h])
-        mat(MB("OXL%d" % h), "OXL%d" % h, Xm, "XI", "OXl", None, ["n0", "rho"][h])
+    mms([(T.K0[:, 0:128], MB("ICO%d" % j) if j else MB("IB"), T.FB[:, 128 * j:128 * j + 128], j == 0, j == 5) for j in range(6)],
+        ["FB", "IB"] + ["ICO%d" % j for j in range(1, 6)], ["K0.h"], ["K0"])
     cp("V", T.HB[:], T.K0[:, 0:128], ["K0.h"], ["HB"], ["K0"])
-    lo = T.FB[:, 768:896]
+    low = T.FB[:, 768:896]
     for h, bank in ((0, "RV"), (1, "NP")):
-        mms([(T[bank][:, 0:128], MB("OXH%d" % h), T.HB[:], True, False), (T[bank][:, 0:128], MB("OXL%d" % h), lo, False, True)],
+        mms([(T[bank][:, 0:128], MB("OXH%d" % h), T.HB[:], True, False), (T[bank][:, 0:128], MB("OXL%d" % h), low, False, True)],
             ["HB", "FB", "OXH%d" % h, "OXL%d" % h], [bank + ".x"], [bank])
-    mat(MB("PERM64"), "PERM64", Xm, "XI", "PERMh", 64.0)
-    mat(MB("PERM1"), "PERM1", Xm, "XI", "PERMh", 1.0)
     for h, bank in ((0, "RV"), (1, "NP")):
         for b in (0, 1):
             c0 = 256 * me + 128 * b + 64 * h
@@ -255,7 +259,12 @@ def rank_program(g, core, T, topo):
     forward("i", "LO", "LOi", 256)
     forward("1", "LW", "LW1", 128)
 
-    mms([(T.K1[:, 0:128], MB("PERM64"), T.HB[:], True, False), (T.K1[:, 0:128], MB("PERM1"), lo, False, True)],
+    lin("pa", "h3", -16, "X0")
+    lin("pb", "rho", 8, "pa")
+    lin("PERMh", "pb", 1, 16.0)
+    mat(MB("PERM1"), "PERM1", Xm, "XI", "PERMh", 1.0)
+    sc(MB("PERM64"), MB("PERM1"), 64.0, ["PERM1"], ["PERM64"])
+    mms([(T.K1[:, 0:128], MB("PERM64"), T.HB[:], True, False), (T.K1[:, 0:128], MB("PERM1"), low, False, True)],
         ["HB", "FB", "PERM64", "PERM1"], ["K1.o"], ["K1"])
     cp("V", T.OF[:], T.K1[:, 0:128], ["K1.o"], ["OF0", "OF1"], ["K1"])
     cp("V", T.OL[:], T.OF[:], ["OF0", "OF1"], ["OL0", "OL1"])
@@ -265,33 +274,31 @@ def rank_program(g, core, T, topo):
     for p in range(4):
         lin("kr%d" % p, "k", 1, -32.0 * p)
         mat(MB("REP%d" % p), "REP%d" % p, fld("f31"), "f31", "kr%d" % p, 1.0)
-        if p >= 4 - NREP:
-            mat(MX("REPF%d" % p), "REPF%d" % p, fld("f31"), "f31", "kr%d" % p, 1.0)
+        if p >= 4 - max(max(n) for n in NREP.values()):
+            sc(MX("REPF%d" % p), MB("REP%d" % p), 1.0, ["REP%d" % p], ["REPF%d" % p])
     emit("V", [lambda: g.vector.memset(T.W[:, 8192:8200], -BIG)], (), ["Wz"])
     lin("sent", "h3", -128, 128.0)
     emit("V", [lambda: g.vector.memset(MB("ONES"), 1.0)], (), ["ONES"])
-    ts(T.OT[:, 8192:8208], T.MBF[:, 128 * MATB.index("ONES"):128 * MATB.index("ONES") + 16], col("sent"), A.mult, None, None, ["ONES", "c_sent"], ["OTz"])
+    ones = 128 * MATB.index("ONES")
+    ts(T.OT[:, 8192:8208], T.MBF[:, ones:ones + 16], col("sent"), A.mult, None, None, ["ONES", "c_sent"], ["OTz"])
     ts(T.MK[:], T.MKI[:], col("s"), A.is_equal, None, None, ["MKI", "c_s"], ["MK"])
     lin("own15", "grp", 16, 15.0)
     lin("ot", "rho", -32, "own15")
     lin("oth15", "ot", 1, 16.0)
     lin("w64", "h3", -63, 64.0)
-    Xs = T.XI[:]
     mat(SL("BKO"), "BKO", Xs, "XI", "own15", None, "w64")
     mat(SL("BKX"), "BKX", Xs, "XI", "oth15", None, "w64")
 
     def late():
+        emit("V", [lambda: g.vector.memset(T.MSL[:, 0:4], 0.0), lambda: g.vector.memset(T.MSL[:, 148:160], 0.0)], (), ["GUARD"])
         mat(SL("OWN"), "OWN", Xs, "XI", "own15", 1.0)
         mat(SL("OTH"), "OTH", Xs, "XI", "oth15", 1.0)
+        sc(T.MX[:, 0:152], T.MSL[:, 0:152], 32.0, ["OWN", "GUARD"], ["MX0"])
         for j, d in enumerate(DELTA):
-            lin("d%d" % j, "own15", 1, float(d))
-            mat(SL("BD%d" % j), "BD%d" % j, Xs, "XI", "d%d" % j, -1.0)
-        ts(T.MX[:, 0:144], SL("OWN"), 32.0, A.mult, None, None, ["OWN"], ["MX0"])
-        for j in range(6):
-            tt(SL("BD%d" % j), SL("BD%d" % j), T.MX[:, 0:144], A.add, ["MX0"], ["BD%d" % j])
+            k0 = 160 + 144 * SLID.index("BD%d" % j)
+            tt(T.MSL[:, k0:k0 + 144], T.MX[:, 4:148], T.MSL[:, 4 - d:148 - d], A.subtract, ["MX0", "OWN", "GUARD"], ["BD%d" % j])
         lin("thr1", "b0", 1, -0.5)
         lin("thr2", "b1", 1, -0.5)
-        mat(MB("IB"), "IB", Xm, "XI", "k", 1.0)
         mat(MB("E8"), "E8", fld("f8"), "f8", "blk", -2.0)
         ts(MB("GT"), Xm, col("k"), A.is_gt, None, None, ["XI", "c_k"], ["GT"])
         tt(MB("E8"), MB("E8"), MB("GT"), A.mult, ["GT"], ["E8"])
@@ -299,38 +306,37 @@ def rank_program(g, core, T, topo):
         lin("bf", "rho", -4, "blk")
         lin("blkf", "bf", 1, 2.0)
         mat(MX("CH"), "CH", fld("f8"), "f8", "blkf", 1.0)
+
+    def late2():
         lin("ta", "rho", -16, "X0")
         lin("T0", "ta", 1, 16.0)
         lin("T8", "ta", 1, 24.0)
         mat(MB("ENT0"), "ENT0", Xm, "XI", "T0", None, "w64")
         mat(MB("ENT1"), "ENT1", Xm, "XI", "T8", None, "w64")
-        mat(MB("KEEPN"), "KEEPN", Xm, "XI", "k", -16384.0)
+        sc(MB("KEEPN"), MB("IB"), -16384.0, ["IB"], ["KEEPN"])
         lin("g0", "h3", -1, 1.0)
         for h, gn in ((0, "g0"), (1, "h3")):
             lin("a%d" % h, gn, -BIG, 0.0)
-            lin("q%d" % h, gn, -256, 0.0)
             mat(MB("ANY%d" % h), "ANY%d" % h, fld("f16"), "f16", "grp", None, "a%d" % h)
             mat(MB("KX%d" % h), "KX%d" % h, fld("f119"), "f119", "T0", None, gn)
-            mat(MB("KN%d" % h), "KN%d" % h, fld("f119"), "f119", "T0", None, "q%d" % h)
+            sc(MB("KN%d" % h), MB("KX%d" % h), -256.0, ["KX%d" % h], ["KN%d" % h])
         lin("sa", "rho", -32, "k")
         lin("SWh", "sa", 1, 16.0)
         mat(MX("SW"), "SW", Xm, "XI", "SWh", 1.0)
-        mat(MX("NSW"), "NSW", Xm, "XI", "SWh", -1.0)
-        mat(MX("IF"), "IF", Xm, "XI", "k", 1.0)
-        tt(MX("ISW"), MX("SW"), MX("IF"), A.add, ["SW", "IF"], ["ISW"])
+        sc(MX("NSW"), MX("SW"), -1.0, ["SW"], ["NSW"])
+        tt(MX("ISW"), MX("SW"), MB("IB"), A.add, ["SW", "IB"], ["ISW"])
         lin("temp", "i", 1024, 0.0)
         names.append("kz")
         ts(col("kz"), col("k"), 0.0, A.is_equal, -1024.0, A.mult, ["c_k"], ["c_kz"])
-        lin("kp", "kz", -1, 0.0)
         ts(MB("TMN"), fld("f15"), col("kz"), A.mult, None, None, ["f15", "c_kz"], ["TMN"])
-        ts(MB("TMP"), fld("f15"), col("kp"), A.mult, None, None, ["f15", "c_kp"], ["TMP"])
+        sc(MB("TMP"), MB("TMN"), -1.0, ["TMN"], ["TMP"])
         emit("V", [lambda: g.vector.memset(T.RS[:], 0.0)], (), ["RS"])
         emit("V", [lambda: g.vector.memset(T.RS[:, 0::8], -BIG)], (), ["RS"])
         lin("iv", "rho", -8, "OXn")
         lin("INVh", "iv", 1, 8.0)
         mat(MX("INVF"), "INVF", Xm, "XI", "INVh", 1.0)
         for j, c in enumerate([-4032.0, -768.0, 512.0, 1920.0, 64.0]):
-            mat(MB("INV%d" % j), "INV%d" % j, Xm, "XI", "INVh", c)
+            sc(MB("INV%d" % j), MX("INVF"), c, ["INVF"], ["INV%d" % j])
 
     OTALL = ["OTz"] + ["OT%d%d%d" % (b, p, h) for b in (0, 1) for p in range(4) for h in (0, 1)]
     WALL = ["Wz"] + ["W%d%d%d" % (b, p, h) for b in (0, 1) for p in range(4) for h in (0, 1)]
@@ -352,13 +358,13 @@ def rank_program(g, core, T, topo):
             cp(qs[p % len(qs)], T.OT[:, d0:d0 + 512], out, [bank + ".r"], ["OT%d%d%d" % (b, p, h)], [bank])
 
     def rep_w_dma(x, b, h):
-        n = 4 - NREP
+        n = 4 - NREP[x][h != half]
         dmas("Y", [(T.W[32 * pp:32 * pp + 32, 4096 * b + 1024 * p + 512 * h:4096 * b + 1024 * p + 512 * h + 512],
                     T["LW" + x][32 * p:32 * p + 32, 512 * h:512 * h + 512]) for p in range(n) for pp in range(4)],
-             "dW%s%d" % (x, h), have("LW", x, h), ["W%d%d%d" % (b, p, h) for p in range(n)])
+             "dW%s%d" % (x, h), have("LW", x, h) + (have("LO", "i", half) if x == "0" else []), ["W%d%d%d" % (b, p, h) for p in range(n)])
 
     def rep_w_pe(x, b, h, q):
-        for p in range(4 - NREP, 4):
+        for p in range(4 - NREP[x][h != half], 4):
             buf, c0, bank = rb[nb[0] % 4]
             nb[0] += 1
             out = T[buf][:, c0:c0 + 512]
@@ -384,13 +390,14 @@ def rank_program(g, core, T, topo):
         ts(T.HAS[:], T.OF[:, 64 * b:64 * b + 64], 8191.5, A.is_lt, None, None, ["OF%d" % b], ["HAS"])
         cp("V", T.KL[:, 64:128], T.K1[:, 0:64], ["K1.k"], ["KL1"], ["K1"])
 
-    def natural(b):
-        o = T.OF[:, 64 * b:64 * b + 64]
-        cp("V", T.YI[:], o, ["OF%d" % b], ["YI"])
+    def fields(b):
+        cp("V", T.YI[:], T.OF[:, 64 * b:64 * b + 64], ["OF%d" % b], ["YI"])
         for j, (sh, m) in enumerate([(12, 1), (10, 3), (9, 1), (7, 3), (6, 1)]):
             ts(T.YFI[:, 64 * j:64 * j + 64], T.YI[:], sh, A.logical_shift_right, m, A.bitwise_and, ["YI"], ["YFI%d" % j])
         cp("V", T.YFB[:], T.YFI[:], ["YFI%d" % j for j in range(5)], ["YFB"])
-        mms([(T.YY[:, 128:192], MX("INVF"), o, True, False)]
+
+    def natural(b):
+        mms([(T.YY[:, 128:192], MX("INVF"), T.OF[:, 64 * b:64 * b + 64], True, False)]
             + [(T.YY[:, 128:192], MB("INV%d" % j), T.YFB[:, 64 * j:64 * j + 64], False, j == 4) for j in range(5)],
             ["OF%d" % b, "YFB", "INVF"] + ["INV%d" % j for j in range(5)], ["YY.n"], ["YY"])
         cp("S", T["YO%d" % b][:], T.YY[:, 128:192], ["YY.n"], ["YO%d" % b], ["YY"])
@@ -412,17 +419,20 @@ def rank_program(g, core, T, topo):
         tt(T.VX[:], Wt.indirect(T.KL[:, 64:128]), XE[:], A.is_lt, WALL + ["KL1"] + xe, ["VX"])
         mms([(T.RV[:, 0:64], SL("OTH", q), T.VX[:, q::16], False, q == 15) for q in range(16)], ["VX", "OTH"], ["RV.v2"], ["RV"])
         st = {1: [(0, 1, 2)], 2: [(0, 2, 4), (1, 3, 4)], 3: [(0, 3, 4), (1, 2, 4)]}[m]
+        thr = "thr1" if m == 1 else "thr2"
+        nq = 0
         for u, v, s in st:
             for y, z in ((u, v), (v, u)):
                 tt(T.C[:, y::s], T.U[:, y::s], T.UP[:, z::s], A.is_gt, ["U", "UPa.r", "UPb.r"], ["C%d" % y], ["UPa", "UPb"])
-        cs = ["C%d" % y for u, v, s in st for y in (u, v)]
-        thr = "thr1" if m == 1 else "thr2"
-        mms([(T.DD[:, 0:64], SL("BD%d" % DELTA.index((q ^ m) - q), q), T.C[:, q::16], q == 0, q == 15) for q in range(16)],
-            cs + ["BD%d" % j for j in range(6)], ["DD.d"], ["DD"])
+                qs = range(y, 16, s)
+                mms([(T.DD[:, 0:64], SL("BD%d" % DELTA.index((q ^ m) - q), q), T.C[:, q::16], nq + j == 0, nq + j == 15) for j, q in enumerate(qs)],
+                    ["C%d" % y] + ["BD%d" % j for j in range(6)], ["DD.d%d" % y], ["DD"])
+                nq += len(qs)
+        dd = ["DD.d%d" % y for u, v, s in st for y in (u, v)]
         ts(T.R1[:], T.RV[:, 0:64], 1024.0, A.mult, col(thr), A.add, ["RV.v", "RV.v2", "c_" + thr], ["R1"], ["RV"])
-        tt(T.REV[:], T.DD[:, 0:64], T.R1[:], A.is_ge, ["DD.d", "R1"], ["REV"], ["DD"])
+        tt(T.REV[:], T.DD[:, 0:64], T.R1[:], A.is_ge, dd + ["R1"], ["REV"], ["DD"])
         mms([(T.YY[:, 0:64], MB("YM"), T.REV[:], True, True)], ["REV", "YM"], ["YY.y"], ["YY"])
-        ts(T.ND[:], T.DD[:, 0:64], col(thr), A.is_ge, None, None, ["DD.d", "c_" + thr], ["ND"], ["DD"])
+        ts(T.ND[:], T.DD[:, 0:64], col(thr), A.is_ge, None, None, dd + ["c_" + thr], ["ND"], ["DD"])
         tt(T.NH[:], T.ND[:], T.HAS[:], A.mult, ["ND", "HAS"], ["NH"])
         ts(T.FF[:], T.YY[:, 0:64], 0.5, A.is_gt, None, None, ["YY.y"], ["FF"], ["YY"])
         tt(T.FK[:], T.FF[:], T.KC[:], A.mult, ["FF", "KC"], ["FK"])
@@ -442,8 +452,7 @@ def rank_program(g, core, T, topo):
         cp("V", ol, n, ["OF%d" % b], ["OL%d" % b])
         for h, bank in ((0, "K0"), (1, "K1")):
             mms([(T[bank][:, 0:64], MX("NSW"), T["LW" + x][:, 128 * me + 64 * h:128 * me + 64 * h + 64], True, False),
-                 (T[bank][:, 0:64], MB("TMN"), MB("ONES")[:, 0:64] if False else T.MBF[:, 128 * MATB.index("ONES"):128 * MATB.index("ONES") + 64], False, False)],
-                [mine + "0", mine + "1", "NSW", "TMN", "ONES"], [bank + ".a"], [bank])
+                 (T[bank][:, 0:64], MB("TMN"), T.MBF[:, ones:ones + 64], False, False)], [mine + "0", mine + "1", "NSW", "TMN", "ONES"], [bank + ".a"], [bank])
         emit("S", [lambda: g.scalar.activation(out=T.U5[:, 512:1024], in_=Wt.indirect(T.OL[:, 64 * b + 32:64 * b + 64]), func=AF.Copy)],
              WALL + ["OL%d" % b], ["U51"])
         emit("V", [lambda: g.vector.tensor_copy(out=T.U5[:, 0:512], in_=Wt.indirect(T.OL[:, 64 * b:64 * b + 32]))], WALL + ["OL%d" % b], ["U50"])
@@ -470,6 +479,8 @@ def rank_program(g, core, T, topo):
         mms([(T.NP[:, 256:384], MB("TMP"), MB("ONES"), True, False)], ["TMP", "ONES"], ["NP.t"], ["NP"])
         mms([(T.RV[:, 256:384], MX("ISW"), T.OWNW[:], True, True)], ["OWN0", "OWN1", "ISW"], ["RV.s"], ["RV"])
         mms([(T.NP[:, 256:384], MX("SW"), T.OWNW[:], False, True)], ["OWN0", "OWN1", "SW"], ["NP.t2"], ["NP"])
+        if not nx:
+            fields(b)
         ts(T.M1[:], T.RV[:, 256:384], 0.0, A.min, col("n0"), A.add, ["RV.s", "c_n0"], ["M1"], ["RV"])
         ts(T.M2[:], T.M1[:], 1, A.arith_shift_right, None, None, ["M1"], ["M2"])
         if nx:
@@ -483,34 +494,32 @@ def rank_program(g, core, T, topo):
             src, sr = T.NF[:], ["NF"]
         if t > 0:
             ts(T["YW%d" % b][:], src, col("temp"), A.add, col("sgn"), A.mult, sr + ["c_temp", "c_sgn"], ["YW%d" % b])
-            outs = [[], []]
-            for P in range(4):
-                for h in (0, 1):
-                    r0 = 32 * P + 16 * h
-                    outs[0].append((T.yl[r0:r0 + 16, 64 * b:64 * b + 64], T["YW%d" % b][32 * P:32 * P + 16, 64 * h:64 * h + 64]))
-                    outs[1].append((T.yr[r0:r0 + 16, 64 * b:64 * b + 64], T["YW%d" % b][32 * P + 16:32 * P + 32, 64 * h:64 * h + 64]))
-            for q, o in (("Y", outs[0]), ("S", outs[1])):
+            for q, y, r0 in (("Y", T.yl, 0), ("S", T.yr, 16)):
                 pre(q, ["YW%d" % b], [])
-                for d, s in o:
-                    eng[q].dma_start(out=d, in_=s).then_inc(T.sem["dY%d" % b], 16)
+                for P in range(4):
+                    for h in (0, 1):
+                        eng[q].dma_start(out=y[32 * P + 16 * h:32 * P + 16 * h + 16, 64 * b:64 * b + 64],
+                                         in_=T["YW%d" % b][32 * P + r0:32 * P + r0 + 16, 64 * h:64 * h + 64]).then_inc(T.sem["dY%d" % b], 16)
             toks_all["dY%d" % b] = 16 * 16
+            if nx:
+                fields(b)
             natural(b)
 
     hs = [half, 1 - half]
     expand("0", 0)
-    for h in hs:
-        rep_w_dma("0", 0, h)
-    for b in (0, 1):
-        rep_o("i", b, hs[0], "VS")
-    for h in hs:
-        rep_w_pe("0", 0, h, "S")
+    rep_w_pe("0", 0, hs[0], "S")
     late()
     for b in (0, 1):
+        rep_o("i", b, hs[0], "S")
+    for x, b in (("0", 0), ("1", 1)):
+        for h in hs:
+            rep_w_dma(x, b, h)
+    for b in (0, 1):
         rep_o("i", b, hs[1], "VS")
-    for h in hs:
-        rep_w_dma("1", 1, h)
     lists_gather(0)
+    rep_w_pe("0", 0, hs[1], "S")
     lists(0)
+    late2()
     for h in hs:
         rep_w_pe("1", 1, h, "S")
     round_(0)
@@ -524,8 +533,6 @@ def rank_program(g, core, T, topo):
         rep_w_pe(x, b, hs[0], "S")
         lists(t)
         rep_w_pe(x, b, hs[1], "S")
-        if t == 1:
-            pass
         round_(t)
         if t == 1:
             expand("2", 0)

@@ -3,47 +3,30 @@ from concourse.mybir import AluOpType as A, ActivationFunctionType as AF
 
 EXW = ["0", "1", "2", "3"]
 EXO = ["i", "2", "3"]
-NREP = {"0": (2, 2), "1": (1, 1), "2": (1, 2), "3": (1, 2)}
+NREP = {"0": (2, 1), "1": (1, 1), "2": (1, 1), "3": (1, 1)}
 FREE = ["LW0", "LOi", "LW1", "LO2", "LO3"]
 BIG = 2.0 ** 23
 MATB = (["REP%d" % p for p in range(4)] + ["YM", "E8", "GT", "ENT0", "ENT1", "KEEPN", "ANY0", "ANY1", "KX0", "KX1", "KN0", "KN1", "IB",
         "TMN", "TMP", "ONES", "PERM64", "PERM1", "OXH0", "OXH1", "OXL0", "OXL1"]
         + ["ICO%d" % f for f in range(6)] + ["INV%d" % f for f in range(5)])
-MATF = ["REPF%d" % p for p in range(4)] + ["CH", "SW", "NSW", "ISW", "INVF"]
-SLID = ["OTH", "BKO", "BKX"] + ["BD%d" % d for d in range(6)]
+MATF = ["REPF%d" % p for p in range(4)] + ["CH0", "CH1", "SW", "NSW", "ISW", "INVF"]
+SLID = ["OTH", "BKO"] + ["BD%d" % d for d in range(6)]
 DELTA = [1, -1, 2, -2, 3, -3]
-
-SCRATCH = {
-    "W": ("sbuf", [128, 8200], "float32"), "OT": ("sbuf", [128, 8208], "bfloat16"),
-    "MBF": ("sbuf", [128, 128 * len(MATB)], "bfloat16"), "MFF": ("sbuf", [128, 128 * len(MATF)], "float32"),
-    "MSL": ("sbuf", [128, 144 * len(SLID) + 160], "bfloat16"),
-    "CI": ("sbuf", [128, 16], "int32"), "CF": ("sbuf", [128, 64], "float32"),
-    "XI": ("sbuf", [128, 144], "float32"), "MI": ("sbuf", [128, 128], "int32"), "MF": ("sbuf", [128, 640], "int32"),
-    "MKI": ("sbuf", [128, 1152], "int32"), "MK": ("sbuf", [128, 1152], "bfloat16"), "RS": ("sbuf", [128, 512], "float32"),
-    "ST": ("sbuf", [128, 256], "int32"), "OI": ("sbuf", [128, 128], "int32"),
-    "FI": ("sbuf", [128, 896], "int32"), "FB": ("sbuf", [128, 896], "bfloat16"), "HB": ("sbuf", [128, 128], "bfloat16"),
-    "OF": ("sbuf", [128, 128], "float32"), "OL": ("sbuf", [128, 128], "uint16"),
-    "XE0": ("sbuf", [128, 1024], "float32"), "XE1": ("sbuf", [128, 1024], "float32"),
-    "GM": ("sbuf", [128, 1024], "bfloat16"), "KL": ("sbuf", [128, 128], "uint16"), "KC": ("sbuf", [128, 64], "float32"),
-    "HAS": ("sbuf", [128, 64], "float32"), "U": ("sbuf", [128, 1024], "float32"),
-    "VO": ("sbuf", [128, 1024], "bfloat16"), "VX": ("sbuf", [128, 1024], "bfloat16"), "C": ("sbuf", [128, 1024], "bfloat16"),
-    "R1": ("sbuf", [128, 64], "float32"), "REV": ("sbuf", [128, 64], "bfloat16"), "ND": ("sbuf", [128, 64], "float32"),
-    "NH": ("sbuf", [128, 64], "float32"), "FF": ("sbuf", [128, 64], "float32"), "FK": ("sbuf", [128, 64], "float32"),
-    "KEEP": ("sbuf", [128, 64], "bfloat16"), "OK": ("sbuf", [128, 64], "float32"), "CL": ("sbuf", [128, 64], "uint16"),
-    "E": ("sbuf", [128, 1024], "bfloat16"), "OXA": ("sbuf", [128, 128], "bfloat16"),
-    "HN": ("sbuf", [128, 64], "bfloat16"), "U5": ("sbuf", [128, 1024], "float32"), "MX": ("sbuf", [128, 1024], "float32"),
-    "OWNW": ("sbuf", [128, 128], "float32"), "M1": ("sbuf", [128, 128], "int32"), "M2": ("sbuf", [128, 128], "int32"),
-    "NF": ("sbuf", [128, 128], "float32"), "YW0": ("sbuf", [128, 128], "float32"), "YW1": ("sbuf", [128, 128], "float32"),
-    "YI": ("sbuf", [128, 64], "int32"), "YFI": ("sbuf", [128, 320], "int32"), "YFB": ("sbuf", [128, 320], "bfloat16"),
-    "YO0": ("sbuf", [128, 64], "float32"), "YO1": ("sbuf", [128, 64], "float32"),
-    "K0": ("psum", [128, 512], "float32"), "K1": ("psum", [128, 512], "float32"), "RV": ("psum", [128, 512], "float32"),
-    "DD": ("psum", [128, 512], "float32"), "YY": ("psum", [128, 512], "float32"), "NP": ("psum", [128, 512], "float32"),
-    "UP": ("psum", [128, 1024], "float32"),
-}
-for _x in EXW:
-    SCRATCH["LW" + _x] = ("sbuf", [128, 1024], "float32")
-for _x in EXO:
-    SCRATCH["LO" + _x] = ("sbuf", [128, 2048 if _x == "i" else 1024], "bfloat16")
+F, B16, I32, U16 = "float32", "bfloat16", "int32", "uint16"
+SCRATCH = {}
+for _n, _w, _d in (("W", 8200, F), ("OT", 8208, B16), ("MBF", 128 * len(MATB), B16), ("MFF", 128 * len(MATF), F), ("MSL", 144 * len(SLID) + 160, B16),
+                   ("CI", 16, I32), ("CF", 64, F), ("XI", 144, F), ("MI", 128, I32), ("MF", 768, I32), ("MKI", 1152, I32), ("MK", 1152, B16),
+                   ("RS", 640, F), ("ST", 256, I32), ("OI", 128, I32), ("FI", 896, I32), ("FB", 896, B16), ("HB", 128, B16), ("OF", 128, F),
+                   ("OL", 128, U16), ("XE0", 1024, F), ("XE1", 1024, F), ("GM", 1024, B16), ("KL", 128, U16), ("KC", 64, F), ("HAS", 64, F),
+                   ("U", 1024, F), ("VO", 1024, B16), ("VX", 1024, B16), ("C", 1024, B16), ("R1", 64, F), ("REV", 64, B16), ("ND", 64, F),
+                   ("NH", 64, F), ("FF", 64, F), ("FK", 64, F), ("KEEP", 64, B16), ("OK", 64, F), ("CL", 32, U16), ("E", 512, B16),
+                   ("OXA", 128, B16), ("HN", 64, B16), ("U5", 1024, F), ("MX", 1024, F), ("OWNW", 128, F), ("M1", 128, I32), ("M2", 128, I32),
+                   ("NF", 128, F), ("YW0", 128, F), ("YW1", 128, F), ("YI", 64, I32), ("YFI", 320, I32), ("YFB", 320, B16), ("YO0", 64, F),
+                   ("YO1", 64, F), ("LW0", 1024, F), ("LW1", 1024, F), ("LW2", 1024, F), ("LW3", 1024, F), ("LOi", 2048, B16), ("LO2", 1024, B16),
+                   ("LO3", 1024, B16)):
+    SCRATCH[_n] = ("sbuf", [128, _w], _d)
+for _n in ("K0", "K1", "RV", "DD", "YY", "NP", "UP"):
+    SCRATCH[_n] = ("psum", [128, 1024 if _n == "UP" else 512], F)
 SEMAPHORES = (["sV", "sS", "sP", "sG", "dOI", "dST"]
               + [k + "W" + x for x in EXW for k in ("p", "m", "l", "f")] + [k + "O" + x for x in EXO for k in ("p", "m", "l", "f")]
               + ["dW%s%d" % (x, h) for x in EXW for h in (0, 1)] + ["dY0", "dY1", "dO0", "dO1"])
@@ -60,7 +43,6 @@ def rank_program(g, core, T, topo):
     me, half = slot[rank], side[rank]
     peers = [c for r, c in enumerate(cores) if side[r] == half and c != core]
     mate = [c for c in cores if c != core and topo.chip(c) == topo.chip(core)][0]
-
     eng = {"V": g.vector, "S": g.scalar, "P": g.tensor, "G": g, "Y": g.sync}
     cnt, known, clk, wr, rd, bk, toks_all = {q: 0 for q in eng}, {q: {} for q in eng}, {}, {}, {}, {}, {}
 
@@ -155,7 +137,6 @@ def rank_program(g, core, T, topo):
                 eng[q].dma_start(out=T.ST[32 * P + r0:32 * P + r0 + 16, 128 * h:128 * h + 128],
                                  in_=src[32 * P + 16 * h:32 * P + 16 * h + 16, :]).then_inc(T.sem.dST, 16)
     arrive("dST", 16 * 16, ["ST"])
-
     emit("G", [lambda: g.iota(T.CI[:, 0:1], [[0, 1]], 0, 1)], (), ["ci0"])
     emit("G", [lambda: g.iota(T.XI[:], [[1, 144]], 0, 0, allow_small_or_imprecise_dtypes=True)], (), ["XI"])
     emit("G", [lambda: g.iota(T.MI[:], [[1, 128]], 0, 0)], (), ["MI"])
@@ -194,13 +175,11 @@ def rank_program(g, core, T, topo):
     lin("n0", "rho", -1, 1.0, "V")
     for h in (0, 1):
         mat(MB("OXH%d" % h), "OXH%d" % h, Xm, "XI", "OXn", None, ["n0", "rho"][h])
-    lin("OXl", "OXn", 1, 8.0, "V")
-    for h in (0, 1):
-        mat(MB("OXL%d" % h), "OXL%d" % h, Xm, "XI", "OXl", None, ["n0", "rho"][h])
     fi = [(6, 255), (6, 1), (8, 3), (10, 1), (11, 3), (7, 1), (0, 63)]
     for j, (sh, m) in enumerate(fi):
         ts(T.FI[:, 128 * j:128 * j + 128], T.OI[:], sh, A.logical_shift_right, m, A.bitwise_and, ["OI"], ["FI%d" % j])
-    for b in (0, 1):
+
+    def own_walls(b):
         for h in (0, 1):
             ts(T["LW%d" % b][:, 128 * me + 64 * h:128 * me + 64 * h + 64], T.ST[:, 128 * h + 64 * b:128 * h + 64 * b + 64], col("sgn"), A.mult,
                col("ntemp"), A.add, ["ST", "c_sgn", "c_ntemp"], ["LW%do%d" % (b, h)])
@@ -220,61 +199,63 @@ def rank_program(g, core, T, topo):
         pre("G", [kind + x + "o0", kind + x + "o1", kind + x + "p"], [])
         tag = buf[1] + x
         blk = T[buf][:, 4 * w * half:4 * w * half + 4 * w]
-        rid, pid = topo.addr(mate)[0], topo.addr(mate)[1]
         es = topo.engines(core, mate)
         if kind + x in FREE:
             es = [e for e in es if e not in topo.engines(core, peers[0])]
-        g.remote_dma(blk, blk, T.sem["m" + tag], T.sem["f" + tag], pid, rid, sum(1 << e for e in es))
+        g.remote_dma(blk, blk, T.sem["m" + tag], T.sem["f" + tag], topo.addr(mate)[1], topo.addr(mate)[0], sum(1 << e for e in es))
         toks_all["f" + tag] = len(es)
         arrive("m" + tag, len(es), [kind + x + "m"])
 
     def have(kind, x, h):
         return [kind + x + "o0", kind + x + "o1", kind + x + "p"] if h == half else [kind + x + "m"]
 
+    own_walls(0)
     send("0", "LW", "LW0", 128)
-
-    flds = [("f8", 3, 31), ("f16", 4, 15), ("f31", 0, 31), ("f15", 0, 15), ("f119", 0, 119)]
+    flds = [("f8", 3, 31), ("f16", 4, 15), ("f31", 0, 31), ("f15", 0, 15), ("f119", 0, 119), ("f4", 2, 31)]
 
     def fld(n):
         j = [x[0] for x in flds].index(n)
         return T.MF[:, 128 * j:128 * j + 128]
 
-    cp("V", T.FB[:], T.FI[:], ["FI%d" % j for j in range(7)], ["FB"])
+    cp("V", T.FB[:, 0:768], T.FI[:, 0:768], ["FI%d" % j for j in range(6)], ["FB"])
     mms([(T.K0[:, 0:128], MB("ICO%d" % j) if j else MB("IB"), T.FB[:, 128 * j:128 * j + 128], j == 0, j == 5) for j in range(6)],
         ["FB", "IB"] + ["ICO%d" % j for j in range(1, 6)], ["K0.h"], ["K0"])
+    cp("V", T.FB[:, 768:896], T.FI[:, 768:896], ["FI6"], ["FB6"])
+    lin("OXl", "OXn", 1, 8.0, "V")
+    for h in (0, 1):
+        mat(MB("OXL%d" % h), "OXL%d" % h, Xm, "XI", "OXl", None, ["n0", "rho"][h])
     cp("V", T.HB[:], T.K0[:, 0:128], ["K0.h"], ["HB"], ["K0"])
     low = T.FB[:, 768:896]
     for h, bank in ((0, "RV"), (1, "NP")):
         mms([(T[bank][:, 0:128], MB("OXH%d" % h), T.HB[:], True, False), (T[bank][:, 0:128], MB("OXL%d" % h), low, False, True)],
-            ["HB", "FB", "OXH%d" % h, "OXL%d" % h], [bank + ".x"], [bank])
+            ["HB", "FB6", "OXH%d" % h, "OXL%d" % h], [bank + ".x"], [bank])
     for h, bank in ((0, "RV"), (1, "NP")):
         for b in (0, 1):
             c0 = 256 * me + 128 * b + 64 * h
             cp("V" if h == 0 else "S", T.LOi[:, c0:c0 + 64], T[bank][:, 64 * b:64 * b + 64], [bank + ".x"], ["LOio%d" % h + ("b" if b else "")], [bank])
     for h in (0, 1):
         wr["LOio%d" % h] = wr["LOio%d" % h] + wr["LOio%db" % h]
+    own_walls(1)
     send("i", "LO", "LOi", 256)
     send("1", "LW", "LW1", 128)
     forward("0", "LW", "LW0", 128)
     forward("i", "LO", "LOi", 256)
     forward("1", "LW", "LW1", 128)
-
     lin("pa", "h3", -16, "X0")
     lin("pb", "rho", 8, "pa")
     lin("PERMh", "pb", 1, 16.0)
     mat(MB("PERM1"), "PERM1", Xm, "XI", "PERMh", 1.0)
     sc(MB("PERM64"), MB("PERM1"), 64.0, ["PERM1"], ["PERM64"])
     mms([(T.K1[:, 0:128], MB("PERM64"), T.HB[:], True, False), (T.K1[:, 0:128], MB("PERM1"), low, False, True)],
-        ["HB", "FB", "PERM64", "PERM1"], ["K1.o"], ["K1"])
+        ["HB", "FB6", "PERM64", "PERM1"], ["K1.o"], ["K1"])
     cp("V", T.OF[:], T.K1[:, 0:128], ["K1.o"], ["OF0", "OF1"], ["K1"])
     cp("V", T.OL[:], T.OF[:], ["OF0", "OF1"], ["OL0", "OL1"])
-
     for j, (n, sh, m) in enumerate(flds):
         ts(fld(n), T.MI[:], sh, A.logical_shift_right, m, A.bitwise_and, ["MI"], [n])
     for p in range(4):
         lin("kr%d" % p, "k", 1, -32.0 * p)
         mat(MB("REP%d" % p), "REP%d" % p, fld("f31"), "f31", "kr%d" % p, 1.0)
-        if p >= 4 - max(max(n) for n in NREP.values()):
+        if p >= 2:
             sc(MX("REPF%d" % p), MB("REP%d" % p), 1.0, ["REP%d" % p], ["REPF%d" % p])
     emit("V", [lambda: g.vector.memset(T.W[:, 8192:8200], -BIG)], (), ["Wz"])
     lin("sent", "h3", -128, 128.0)
@@ -283,15 +264,17 @@ def rank_program(g, core, T, topo):
     ts(T.OT[:, 8192:8208], T.MBF[:, ones:ones + 16], col("sent"), A.mult, None, None, ["ONES", "c_sent"], ["OTz"])
     ts(T.MK[:], T.MKI[:], col("s"), A.is_equal, None, None, ["MKI", "c_s"], ["MK"])
     lin("own15", "grp", 16, 15.0)
-    lin("ot", "rho", -32, "own15")
-    lin("oth15", "ot", 1, 16.0)
     lin("w64", "h3", -63, 64.0)
     mat(SL("BKO"), "BKO", Xs, "XI", "own15", None, "w64")
-    mat(SL("BKX"), "BKX", Xs, "XI", "oth15", None, "w64")
+    lin("sa", "rho", -32, "k")
+    lin("SWh", "sa", 1, 16.0)
+    mat(MX("SW"), "SW", Xm, "XI", "SWh", 1.0)
 
     def late():
         emit("V", [lambda: g.vector.memset(T.MSL[:, 0:4], 0.0), lambda: g.vector.memset(T.MSL[:, 148:160], 0.0)], (), ["GUARD"])
         mat(SL("OWN"), "OWN", Xs, "XI", "own15", 1.0)
+        lin("ot", "rho", -32, "own15")
+        lin("oth15", "ot", 1, 16.0)
         mat(SL("OTH"), "OTH", Xs, "XI", "oth15", 1.0)
         sc(T.MX[:, 0:152], T.MSL[:, 0:152], 32.0, ["OWN", "GUARD"], ["MX0"])
         for j, d in enumerate(DELTA):
@@ -305,33 +288,39 @@ def rank_program(g, core, T, topo):
         tt(MB("YM"), MB("E8"), MB("IB"), A.add, ["E8", "IB"], ["YM"])
         lin("bf", "rho", -4, "blk")
         lin("blkf", "bf", 1, 2.0)
-        mat(MX("CH"), "CH", fld("f8"), "f8", "blkf", 1.0)
-
-    def late2():
+        lin("bl2", "blkf", 2, 0.0)
+        lin("bl3", "blkf", 2, 1.0)
+        mat(MX("CH0"), "CH0", fld("f4"), "f4", "bl2", 1.0)
+        mat(MX("CH1"), "CH1", fld("f4"), "f4", "bl3", 1.0)
         lin("ta", "rho", -16, "X0")
         lin("T0", "ta", 1, 16.0)
         lin("T8", "ta", 1, 24.0)
+        lin("g0", "h3", -1, 1.0)
+        lin("a0", "g0", -BIG, 0.0)
+        lin("a1", "h3", -BIG, 0.0)
+        lin("temp", "i", 1024, 0.0)
         mat(MB("ENT0"), "ENT0", Xm, "XI", "T0", None, "w64")
         mat(MB("ENT1"), "ENT1", Xm, "XI", "T8", None, "w64")
-        sc(MB("KEEPN"), MB("IB"), -16384.0, ["IB"], ["KEEPN"])
-        lin("g0", "h3", -1, 1.0)
         for h, gn in ((0, "g0"), (1, "h3")):
-            lin("a%d" % h, gn, -BIG, 0.0)
             mat(MB("ANY%d" % h), "ANY%d" % h, fld("f16"), "f16", "grp", None, "a%d" % h)
             mat(MB("KX%d" % h), "KX%d" % h, fld("f119"), "f119", "T0", None, gn)
-            sc(MB("KN%d" % h), MB("KX%d" % h), -256.0, ["KX%d" % h], ["KN%d" % h])
-        lin("sa", "rho", -32, "k")
-        lin("SWh", "sa", 1, 16.0)
-        mat(MX("SW"), "SW", Xm, "XI", "SWh", 1.0)
-        sc(MX("NSW"), MX("SW"), -1.0, ["SW"], ["NSW"])
+
+    def late2():
         tt(MX("ISW"), MX("SW"), MB("IB"), A.add, ["SW", "IB"], ["ISW"])
-        lin("temp", "i", 1024, 0.0)
         names.append("kz")
         ts(col("kz"), col("k"), 0.0, A.is_equal, -1024.0, A.mult, ["c_k"], ["c_kz"])
         ts(MB("TMN"), fld("f15"), col("kz"), A.mult, None, None, ["f15", "c_kz"], ["TMN"])
-        sc(MB("TMP"), MB("TMN"), -1.0, ["TMN"], ["TMP"])
         emit("V", [lambda: g.vector.memset(T.RS[:], 0.0)], (), ["RS"])
         emit("V", [lambda: g.vector.memset(T.RS[:, 0::8], -BIG)], (), ["RS"])
+
+    def late2s():
+        sc(MB("KEEPN"), MB("IB"), -16384.0, ["IB"], ["KEEPN"])
+        for h in (0, 1):
+            sc(MB("KN%d" % h), MB("KX%d" % h), -256.0, ["KX%d" % h], ["KN%d" % h])
+        sc(MX("NSW"), MX("SW"), -1.0, ["SW"], ["NSW"])
+        sc(MB("TMP"), MB("TMN"), -1.0, ["TMN"], ["TMP"])
+
+    def late3():
         lin("iv", "rho", -8, "OXn")
         lin("INVh", "iv", 1, 8.0)
         mat(MX("INVF"), "INVF", Xm, "XI", "INVh", 1.0)
@@ -339,7 +328,7 @@ def rank_program(g, core, T, topo):
             sc(MB("INV%d" % j), MX("INVF"), c, ["INVF"], ["INV%d" % j])
 
     OTALL = ["OTz"] + ["OT%d%d%d" % (b, p, h) for b in (0, 1) for p in range(4) for h in (0, 1)]
-    WALL = ["Wz"] + ["W%d%d%d" % (b, p, h) for b in (0, 1) for p in range(4) for h in (0, 1)]
+    WALL = ["Wz"] + ["W%d%d%d" % (b, p, h) + z for b in (0, 1) for p in range(4) for h in (0, 1) for z in ("", "s")]
     rb = [("UP", 0, "UPa"), ("UP", 512, "UPb"), ("YY", 0, "YY"), ("DD", 0, "DD")]
     nb = [0]
 
@@ -360,8 +349,13 @@ def rank_program(g, core, T, topo):
     def rep_w_dma(x, b, h):
         n = 4 - NREP[x][h != half]
         dmas("Y", [(T.W[32 * pp:32 * pp + 32, 4096 * b + 1024 * p + 512 * h:4096 * b + 1024 * p + 512 * h + 512],
-                    T["LW" + x][32 * p:32 * p + 32, 512 * h:512 * h + 512]) for p in range(n) for pp in range(4)],
+                    T["LW" + x][32 * p:32 * p + 32, 512 * h:512 * h + 512]) for p in range(n) for pp in range(4) if pp != p],
              "dW%s%d" % (x, h), have("LW", x, h) + (have("LO", "i", half) if x == "0" else []), ["W%d%d%d" % (b, p, h) for p in range(n)])
+
+    def rep_w_same(x, b, h, q):
+        for p in range(4 - NREP[x][h != half]):
+            d0 = 4096 * b + 1024 * p + 512 * h
+            cp(q, T.W[32 * p:32 * p + 32, d0:d0 + 512], T["LW" + x][32 * p:32 * p + 32, 512 * h:512 * h + 512], have("LW", x, h), ["W%d%d%ds" % (b, p, h)])
 
     def rep_w_pe(x, b, h, q):
         for p in range(4 - NREP[x][h != half], 4):
@@ -383,12 +377,12 @@ def rank_program(g, core, T, topo):
 
     def lists(t):
         b = t & 1
-        for n, bank in (("BKO", "K0"), ("BKX", "K1")):
-            mms([(T[bank][:, 0:64], SL(n, q), T.GM[:, q::16], q == 0, q == 15) for q in range(16)], ["GM", n], [bank + ".k"], [bank])
-        cp("V", T.KL[:, 0:64], T.K0[:, 0:64], ["K0.k"], ["KL0"], ["K0"])
+        mms([(T.K0[:, 0:64], SL("BKO", q), T.GM[:, q::16], q == 0, q == 15) for q in range(16)], ["GM", "BKO"], ["K0.k"], ["K0"])
         ts(T.KC[:], T.K0[:, 0:64], -8192.0, A.add, None, None, ["K0.k"], ["KC"], ["K0"])
+        mms([(T.K1[:, 0:64], MX("SW"), T.KC[:], True, True)], ["KC", "SW"], ["K1.k"], ["K1"])
+        cp("V", T.KL[:, 0:64], T.K0[:, 0:64], ["K0.k"], ["KL0"], ["K0"])
         ts(T.HAS[:], T.OF[:, 64 * b:64 * b + 64], 8191.5, A.is_lt, None, None, ["OF%d" % b], ["HAS"])
-        cp("V", T.KL[:, 64:128], T.K1[:, 0:64], ["K1.k"], ["KL1"], ["K1"])
+        ts(T.KL[:, 64:128], T.K1[:, 0:64], 8192.0, A.add, None, None, ["K1.k"], ["KL1"], ["K1"])
 
     def fields(b):
         cp("V", T.YI[:], T.OF[:, 64 * b:64 * b + 64], ["OF%d" % b], ["YI"])
@@ -413,6 +407,8 @@ def rank_program(g, core, T, topo):
         ol = T.OL[:, 64 * b:64 * b + 64]
         emit("S", [lambda: g.scalar.activation(out=T.U[:], in_=Wt.indirect(ol), func=AF.Copy)], WALL + ["OL%d" % b], ["U"])
         cp("S", T.UP[:], T.U[:], ["U"], ["UPa.r", "UPb.r"], ["UPa", "UPb"])
+        if t == 0:
+            late2s()
         XE = T["XE%d" % b]
         tt(T.VO[:], Wt.indirect(T.KL[:, 0:64]), XE[:], A.is_gt, WALL + ["KL0"] + xe, ["VO"])
         mms([(T.RV[:, 0:64], SL("OWN", q), T.VO[:, q::16], q == 0, False) for q in range(16)], ["VO", "OWN"], ["RV.v"], ["RV"])
@@ -436,43 +432,43 @@ def rank_program(g, core, T, topo):
         tt(T.NH[:], T.ND[:], T.HAS[:], A.mult, ["ND", "HAS"], ["NH"])
         ts(T.FF[:], T.YY[:, 0:64], 0.5, A.is_gt, None, None, ["YY.y"], ["FF"], ["YY"])
         tt(T.FK[:], T.FF[:], T.KC[:], A.mult, ["FF", "KC"], ["FK"])
-        mms([(T.YY[:, 64:128], MX("CH"), T.FK[:], True, True)], ["FK", "CH"], ["YY.c"], ["YY"])
+        mms([(T.YY[:, 64:96], MX("CH%d" % e), T.FK[:, 32 * e:32 * e + 32], e == 0, e == 1) for e in (0, 1)], ["FK", "CH0", "CH1"], ["YY.c"], ["YY"])
         tt(T.KEEP[:], T.NH[:], T.FF[:], A.subtract, ["NH", "FF"], ["KEEP"])
         tt(T.OK[:], T.OF[:, 64 * b:64 * b + 64], T.KEEP[:], A.mult, ["OF%d" % b, "KEEP"], ["OK"])
         mms([(T.NP[:, 0:64], MB("KEEPN"), T.KEEP[:], True, False)], ["KEEP", "KEEPN"], ["NP.n"], ["NP"])
-        ts(T.CL[:], T.YY[:, 64:128], 8192.0, A.add, None, None, ["YY.c"], ["CL"], ["YY"])
+        ts(T.CL[:], T.YY[:, 64:96], 8192.0, A.add, None, None, ["YY.c"], ["CL"], ["YY"])
         if nx:
             mms([(T.RV[:, 64 * h + 128:64 * h + 192], MB("KX%d" % h), T.KEEP[:], True, True) for h in (0, 1)], ["KEEP", "KX0", "KX1"], ["RV.k"], ["RV"])
-        emit("V", [lambda: g.vector.tensor_copy(out=T.E[:, 0:512], in_=T.OT[:].indirect(T.CL[:, 0:32]))], OTALL + ["CL"], ["E0"])
-        emit("S", [lambda: g.scalar.activation(out=T.E[:, 512:1024], in_=T.OT[:].indirect(T.CL[:, 32:64]), func=AF.Copy)], OTALL + ["CL"], ["E1"])
-        mms([(T.NP[:, 0:64], MB("ENT0"), T.E[:, 0::16], False, False), (T.NP[:, 0:64], MB("ENT1"), T.E[:, 8::16], False, True)],
+        emit("V", [lambda: g.vector.tensor_copy(out=T.E[:, 0:256], in_=T.OT[:].indirect(T.CL[:, 0:16]))], OTALL + ["CL"], ["E0"])
+        emit("S", [lambda: g.scalar.activation(out=T.E[:, 256:512], in_=T.OT[:].indirect(T.CL[:, 16:32]), func=AF.Copy)], OTALL + ["CL"], ["E1"])
+        mms([(T.NP[:, 32 * e:32 * e + 32], MB("ENT%d" % h), T.E[:, 8 * h + 4 * e::16], False, h == 1 and e == 1) for e in (0, 1) for h in (0, 1)],
             ["E0", "E1", "ENT0", "ENT1"], ["NP.n2"], ["NP"])
+        if nx:
+            old = T.LOi[:, 256 * me + 128 * b:256 * me + 128 * b + 128]
+            tt(T.OXA[:], T.RV[:, 128:256], old, A.mult, ["RV.k", "LOio0", "LOio1"], ["OXA"], ["RV"])
+            for h in (0, 1):
+                mms([(T.DD[:, 128 + 64 * h:192 + 64 * h], MB("KN%d" % h), T.KEEP[:], True, False)]
+                    + [(T.DD[:, 128 + 64 * h + 32 * e:160 + 64 * h + 32 * e], MB("IB"), T.E[:, 8 * h + 4 * e::16], False, e == 1) for e in (0, 1)],
+                    ["KEEP", "E0", "E1", "IB", "KN%d" % h], ["DD.x%d" % h], ["DD"])
         n = T.OF[:, 64 * b:64 * b + 64]
         tt(n, T.NP[:, 0:64], T.OK[:], A.max, ["NP.n", "NP.n2", "OK"], ["OF%d" % b], ["NP"])
         cp("V", ol, n, ["OF%d" % b], ["OL%d" % b])
         for h, bank in ((0, "K0"), (1, "K1")):
             mms([(T[bank][:, 0:64], MX("NSW"), T["LW" + x][:, 128 * me + 64 * h:128 * me + 64 * h + 64], True, False),
                  (T[bank][:, 0:64], MB("TMN"), T.MBF[:, ones:ones + 64], False, False)], [mine + "0", mine + "1", "NSW", "TMN", "ONES"], [bank + ".a"], [bank])
-        emit("S", [lambda: g.scalar.activation(out=T.U5[:, 512:1024], in_=Wt.indirect(T.OL[:, 64 * b + 32:64 * b + 64]), func=AF.Copy)],
+        emit("S", [lambda: g.scalar.activation(out=T.U5[:, 384:1024], in_=Wt.indirect(T.OL[:, 64 * b + 24:64 * b + 64]), func=AF.Copy)],
              WALL + ["OL%d" % b], ["U51"])
-        emit("V", [lambda: g.vector.tensor_copy(out=T.U5[:, 0:512], in_=Wt.indirect(T.OL[:, 64 * b:64 * b + 32]))], WALL + ["OL%d" % b], ["U50"])
-        ts(T.HN[:], n, 8191.5, A.is_lt, None, None, ["OF%d" % b], ["HN"])
-        if nx:
-            old = T.LOi[:, 256 * me + 128 * b:256 * me + 128 * b + 128]
-            for h in (0, 1):
-                mms([(T.DD[:, 128 + 64 * h:192 + 64 * h], MB("KN%d" % h), T.KEEP[:], True, False),
-                     (T.DD[:, 128 + 64 * h:192 + 64 * h], MB("IB"), T.E[:, 8 * h::16], False, True)],
-                    ["KEEP", "E0", "E1", "IB", "KN%d" % h], ["DD.x%d" % h], ["DD"])
-            tt(T.OXA[:], T.RV[:, 128:256], old, A.mult, ["RV.k", "LOio0", "LOio1"], ["OXA"], ["RV"])
-        for h, bank in ((0, "K0"), (1, "K1")):
-            mms([(T[bank][:, 0:64], MB("ANY%d" % h), T.HN[:], False, True)], ["HN", "ANY%d" % h], [bank + ".b"], [bank])
         if nx:
             for h in (0, 1):
                 tt(T["LO" + nx][:, 128 * me + 64 * h:128 * me + 64 * h + 64], T.DD[:, 128 + 64 * h:192 + 64 * h], T.OXA[:, 64 * h:64 * h + 64], A.max,
                    ["DD.x%d" % h, "OXA"], ["LO%so%d" % (nx, h)], ["DD"])
             send(nx, "LO", "LO" + nx, 128)
-        for h in (0, 1):
-            emit("V", [lambda: g.vector.tensor_tensor_scan(out=T.MX[:, 512 * h:512 * h + 512], data0=T.RS[:], data1=T.U5[:, 512 * h:512 * h + 512],
+        emit("V", [lambda: g.vector.tensor_copy(out=T.U5[:, 0:384], in_=Wt.indirect(T.OL[:, 64 * b:64 * b + 24]))], WALL + ["OL%d" % b], ["U50"])
+        ts(T.HN[:], n, 8191.5, A.is_lt, None, None, ["OF%d" % b], ["HN"])
+        for h, bank in ((0, "K0"), (1, "K1")):
+            mms([(T[bank][:, 0:64], MB("ANY%d" % h), T.HN[:], False, True)], ["HN", "ANY%d" % h], [bank + ".b"], [bank])
+        for h, c0, c1 in ((0, 0, 384), (1, 384, 1024)):
+            emit("V", [lambda: g.vector.tensor_tensor_scan(out=T.MX[:, c0:c1], data0=T.RS[:, 0:c1 - c0], data1=T.U5[:, c0:c1],
                                                            initial=-2.0 * BIG, op0=A.add, op1=A.max)], ["RS", "U5%d" % h], ["MX%d" % h])
         for h, bank in ((0, "K0"), (1, "K1")):
             tt(T.OWNW[:, 64 * h:64 * h + 64], T.MX[:, 7 + 8 * h::16], T[bank][:, 0:64], A.max, ["MX0", "MX1", bank + ".a", bank + ".b"], ["OWN%d" % h], [bank])
@@ -481,6 +477,7 @@ def rank_program(g, core, T, topo):
         mms([(T.NP[:, 256:384], MX("SW"), T.OWNW[:], False, True)], ["OWN0", "OWN1", "SW"], ["NP.t2"], ["NP"])
         if not nx:
             fields(b)
+            natural(b)
         ts(T.M1[:], T.RV[:, 256:384], 0.0, A.min, col("n0"), A.add, ["RV.s", "c_n0"], ["M1"], ["RV"])
         ts(T.M2[:], T.M1[:], 1, A.arith_shift_right, None, None, ["M1"], ["M2"])
         if nx:
@@ -503,7 +500,7 @@ def rank_program(g, core, T, topo):
             toks_all["dY%d" % b] = 16 * 16
             if nx:
                 fields(b)
-            natural(b)
+                natural(b)
 
     hs = [half, 1 - half]
     expand("0", 0)
@@ -514,15 +511,20 @@ def rank_program(g, core, T, topo):
     for x, b in (("0", 0), ("1", 1)):
         for h in hs:
             rep_w_dma(x, b, h)
+    rep_w_same("0", 0, hs[0], "S")
     for b in (0, 1):
         rep_o("i", b, hs[1], "VS")
+    rep_w_same("0", 0, hs[1], "S")
     lists_gather(0)
+    rep_w_same("1", 1, hs[0], "V")
     rep_w_pe("0", 0, hs[1], "S")
+    rep_w_pe("1", 1, hs[0], "S")
     lists(0)
+    rep_w_same("1", 1, hs[1], "V")
+    rep_w_pe("1", 1, hs[1], "S")
     late2()
-    for h in hs:
-        rep_w_pe("1", 1, h, "S")
     round_(0)
+    late3()
     expand("1", 1)
     for t, x, b in ((1, "2", 0), (2, "3", 1)):
         for h in hs:
@@ -530,8 +532,10 @@ def rank_program(g, core, T, topo):
         for h in hs:
             rep_o(x, b, h, "VS")
         lists_gather(t)
+        rep_w_same(x, b, hs[0], "S")
         rep_w_pe(x, b, hs[0], "S")
         lists(t)
+        rep_w_same(x, b, hs[1], "S")
         rep_w_pe(x, b, hs[1], "S")
         round_(t)
         if t == 1:

from concourse.bass import DstId, RemoteDMATransfer
from concourse.mybir import AluOpType as A, ActivationFunctionType as AF

EXW = ["0", "1", "2", "3"]
EXO = ["i", "2", "3"]
NREP = {"0": (2, 1), "1": (1, 1), "2": (1, 1), "3": (1, 1)}
FREE = ["LW0", "LOi", "LW1", "LO2", "LO3"]
BIG = 2.0 ** 23
MATB = (["REP%d" % p for p in range(4)] + ["YM", "E8", "GT", "ENT0", "ENT1", "KEEPN", "ANY0", "ANY1", "KX0", "KX1", "KN0", "KN1", "IB",
        "TMN", "TMP", "ONES", "PERM64", "PERM1", "OXH0", "OXH1", "OXL0", "OXL1"]
        + ["ICO%d" % f for f in range(6)] + ["INV%d" % f for f in range(5)])
MATF = ["REPF%d" % p for p in range(4)] + ["CH0", "CH1", "SW", "NSW", "ISW", "INVF"]
SLID = ["OTH", "BKO"] + ["BD%d" % d for d in range(6)]
DELTA = [1, -1, 2, -2, 3, -3]
F, B16, I32, U16 = "float32", "bfloat16", "int32", "uint16"
SCRATCH = {}
for _n, _w, _d in (("W", 8200, F), ("OT", 8208, B16), ("MBF", 128 * len(MATB), B16), ("MFF", 128 * len(MATF), F), ("MSL", 144 * len(SLID) + 160, B16),
                   ("CI", 16, I32), ("CF", 64, F), ("XI", 144, F), ("MI", 128, I32), ("MF", 768, I32), ("MKI", 1152, I32), ("MK", 1152, B16),
                   ("RS", 640, F), ("ST", 256, I32), ("OI", 128, I32), ("FI", 896, I32), ("FB", 896, B16), ("HB", 128, B16), ("OF", 128, F),
                   ("OL", 128, U16), ("XE0", 1024, F), ("XE1", 1024, F), ("GM", 1024, B16), ("KL", 128, U16), ("KC", 64, F), ("HAS", 64, F),
                   ("U", 1024, F), ("VO", 1024, B16), ("VX", 1024, B16), ("C", 1024, B16), ("R1", 64, F), ("REV", 64, B16), ("ND", 64, F),
                   ("NH", 64, F), ("FF", 64, F), ("FK", 64, F), ("KEEP", 64, B16), ("OK", 64, F), ("CL", 32, U16), ("E", 512, B16),
                   ("OXA", 128, B16), ("HN", 64, B16), ("U5", 1024, F), ("MX", 1024, F), ("OWNW", 128, F), ("M1", 128, I32), ("M2", 128, I32),
                   ("NF", 128, F), ("YW0", 128, F), ("YW1", 128, F), ("YI", 64, I32), ("YFI", 320, I32), ("YFB", 320, B16), ("YO0", 64, F),
                   ("YO1", 64, F), ("LW0", 1024, F), ("LW1", 1024, F), ("LW2", 1024, F), ("LW3", 1024, F), ("LOi", 2048, B16), ("LO2", 1024, B16),
                   ("LO3", 1024, B16)):
    SCRATCH[_n] = ("sbuf", [128, _w], _d)
for _n in ("K0", "K1", "RV", "DD", "YY", "NP", "UP"):
    SCRATCH[_n] = ("psum", [128, 1024 if _n == "UP" else 512], F)
SEMAPHORES = (["sV", "sS", "sP", "sG", "dOI", "dST"]
              + [k + "W" + x for x in EXW for k in ("p", "m", "l", "f")] + [k + "O" + x for x in EXO for k in ("p", "m", "l", "f")]
              + ["dW%s%d" % (x, h) for x in EXW for h in (0, 1)] + ["dY0", "dY1", "dO0", "dO1"])


def rank_program(g, core, T, topo):
    rank = T.rank_of(core)
    if rank is None:
        return
    cores = list(T.cores)
    side = [int(topo.die(c) != topo.die(cores[0])) for c in cores]
    slot = [4 * side[r] + sum(1 for q in range(r) if side[q] == side[r]) for r in range(len(cores))]
    assert slot == [4 * (r & 1) + (r >> 1) for r in range(len(cores))]
    me, half = slot[rank], side[rank]
    peers = [c for r, c in enumerate(cores) if side[r] == half and c != core]
    mate = [c for c in cores if c != core and topo.chip(c) == topo.chip(core)][0]
    eng = {"V": g.vector, "S": g.scalar, "P": g.tensor, "G": g, "Y": g.sync}
    cnt, known, clk, wr, rd, bk, toks_all = {q: 0 for q in eng}, {q: {} for q in eng}, {}, {}, {}, {}, {}

    def need(q, toks):
        best = {}
        for s, v in toks:
            best[s] = max(best.get(s, 0), v)
        todo = [(s, v) for s, v in best.items() if known[q].get(s, 0) < v]
        todo = [t for t in todo if not any(o != t and clk[o].get(t[0], 0) >= t[1] for o in todo)]
        for s, v in todo:
            eng[q].wait_ge(T.sem[s], v)
            for a, b in clk[(s, v)].items():
                known[q][a] = max(known[q].get(a, 0), b)
            known[q][s] = max(known[q].get(s, 0), v)

    def pre(q, R, W, B=()):
        toks = []
        for r in R:
            toks += wr.get(r, [])
        for w in W:
            toks += wr.get(w, []) + rd.get(w, [])
        for b in B:
            toks += [t for e, t in bk.get(b, {}).items() if e != q]
        need(q, toks)

    def post(q, tok, R, W, B=()):
        clk[tok] = dict(known[q])
        toks_all[tok[0]] = max(toks_all.get(tok[0], 0), tok[1])
        for r in R:
            rd[r] = [t for t in rd.get(r, []) if t[0] != tok[0]] + [tok]
        for w in W:
            wr[w], rd[w] = [tok], []
        for b in B:
            bk.setdefault(b, {})[q] = tok

    def emit(q, calls, R=(), W=(), B=()):
        pre(q, R, W, B)
        for c in calls:
            c().then_inc(T.sem["s" + q], 1)
            cnt[q] += 1
        post(q, ("s" + q, cnt[q]), R, W, B)

    def dmas(q, pairs, sem, R=(), W=()):
        pre(q, R, W)
        for o, i in pairs:
            eng[q].dma_start(out=o, in_=i).then_inc(T.sem[sem], 16)
        post(q, (sem, 16 * len(pairs)), R, W)

    def arrive(sem, val, W):
        clk[(sem, val)] = {}
        toks_all[sem] = val
        for w in W:
            wr[w] = wr.get(w, []) + [(sem, val)]

    def ts(out, in0, s1, op0, s2=None, op1=None, R=(), W=(), B=()):
        if op1 is None:
            emit("V", [lambda: g.vector.tensor_scalar(out=out, in0=in0, scalar1=s1, scalar2=None, op0=op0)], R, W, B)
        else:
            emit("V", [lambda: g.vector.tensor_scalar(out=out, in0=in0, scalar1=s1, scalar2=s2, op0=op0, op1=op1)], R, W, B)

    def tt(out, a, b, op, R=(), W=(), B=()):
        emit("V", [lambda: g.vector.tensor_tensor(out=out, in0=a, in1=b, op=op)], R, W, B)

    def cp(q, out, i, R=(), W=(), B=()):
        if q == "V":
            emit("V", [lambda: g.vector.tensor_copy(out=out, in_=i)], R, W, B)
        else:
            emit("S", [lambda: g.scalar.activation(out=out, in_=i, func=AF.Copy)], R, W, B)

    def sc(dst, src, scale, R, W):
        emit("S", [lambda: g.scalar.activation(out=dst, in_=src, func=AF.Copy, scale=float(scale))], R, W)

    def mms(groups, R=(), W=(), B=()):
        emit("P", [(lambda m=m: g.tensor.matmul(out=m[0], lhsT=m[1], rhs=m[2], start=m[3], stop=m[4])) for m in groups], R, W, B)

    def MB(n):
        j = MATB.index(n)
        return T.MBF[:, 128 * j:128 * j + 128]

    def MX(n):
        j = MATF.index(n)
        return T.MFF[:, 128 * j:128 * j + 128]

    def SL(n, q=None):
        j = 4 if n == "OWN" else 160 + 144 * SLID.index(n)
        return T.MSL[:, j:j + 144] if q is None else T.MSL[:, j + 15 - q:j + 143 - q]

    dmas("Y", [(T.OI[:], T.opts[:])], "dOI", (), ["OI"])
    for q, r0, src in (("Y", 0, T.lw), ("S", 16, T.rw)):
        for P in range(4):
            for h in (0, 1):
                eng[q].dma_start(out=T.ST[32 * P + r0:32 * P + r0 + 16, 128 * h:128 * h + 128],
                                 in_=src[32 * P + 16 * h:32 * P + 16 * h + 16, :]).then_inc(T.sem.dST, 16)
    arrive("dST", 16 * 16, ["ST"])
    emit("G", [lambda: g.iota(T.CI[:, 0:1], [[0, 1]], 0, 1)], (), ["ci0"])
    emit("G", [lambda: g.iota(T.XI[:], [[1, 144]], 0, 0, allow_small_or_imprecise_dtypes=True)], (), ["XI"])
    emit("G", [lambda: g.iota(T.MI[:], [[1, 128]], 0, 0)], (), ["MI"])
    emit("G", [lambda: g.iota(T.MKI[:], [[0, 9], [1, 8], [0, 16]], 0, 0)], (), ["MKI"])
    ints = [("P", 5, 7), ("rho", 4, 1), ("grp", 4, 15), ("i", 0, 15), ("s", 0, 7), ("h3", 3, 1), ("blk", 3, 31), ("b0", 0, 1), ("b1", 1, 1)]
    for j, (n, sh, m) in enumerate(ints):
        ts(T.CI[:, j + 1:j + 2], T.CI[:, 0:1], sh, A.logical_shift_right, m, A.bitwise_and, ["ci0"], ["ci%d" % (j + 1)])
    names = ["k"] + [x[0] for x in ints]
    cp("V", T.CF[:, 0:10], T.CI[:, 0:10], ["ci%d" % j for j in range(10)], ["c_" + n for n in names])

    def col(n):
        j = names.index(n)
        return T.CF[:, j:j + 1]

    def lin(n, a, m, add, q="S"):
        names.append(n)
        d = add if not isinstance(add, str) else col(add)
        R = ["c_" + a] + (["c_" + add] if isinstance(add, str) else [])
        if q == "S":
            emit("S", [lambda: g.scalar.activation(out=col(n), in_=col(a), func=AF.Identity, bias=d, scale=float(m))], R, ["c_" + n])
        else:
            ts(col(n), col(a), float(m), A.mult, d, A.add, R, ["c_" + n])

    def mat(dst, name, f, fr, h, w, wn=None):
        ts(dst, f, col(h), A.is_equal, w if wn is None else col(wn), A.mult, [fr, "c_" + h] + ([] if wn is None else ["c_" + wn]), [name])

    Xm, Xs = T.XI[:, 0:128], T.XI[:]
    lin("sgn", "rho", 2, -1.0, "V")
    lin("ntemp", "i", -1024, 0.0, "V")
    ico = [1.0, 63.0, 12.0, -8.0, -30.0, -1.0]
    mat(MB("IB"), "IB", Xm, "XI", "k", 1.0)
    for j in range(1, 6):
        sc(MB("ICO%d" % j), MB("IB"), ico[j], ["IB"], ["ICO%d" % j])
    lin("X0", "P", 32, "s", "V")
    lin("OXn", "h3", 16, "X0", "V")
    lin("n0", "rho", -1, 1.0, "V")
    for h in (0, 1):
        mat(MB("OXH%d" % h), "OXH%d" % h, Xm, "XI", "OXn", None, ["n0", "rho"][h])
    fi = [(6, 255), (6, 1), (8, 3), (10, 1), (11, 3), (7, 1), (0, 63)]
    for j, (sh, m) in enumerate(fi):
        ts(T.FI[:, 128 * j:128 * j + 128], T.OI[:], sh, A.logical_shift_right, m, A.bitwise_and, ["OI"], ["FI%d" % j])

    def own_walls(b):
        for h in (0, 1):
            ts(T["LW%d" % b][:, 128 * me + 64 * h:128 * me + 64 * h + 64], T.ST[:, 128 * h + 64 * b:128 * h + 64 * b + 64], col("sgn"), A.mult,
               col("ntemp"), A.add, ["ST", "c_sgn", "c_ntemp"], ["LW%do%d" % (b, h)])

    def send(x, kind, buf, w):
        blk = T[buf][:, w * me:w * me + w]
        pre("G", [kind + x + "o0", kind + x + "o1"], [])
        tag = buf[1] + x
        ids = [DstId(rid=topo.addr(c)[0], pnc=topo.addr(c)[1]) for c in peers]
        g.remote_dma_fused([RemoteDMATransfer(dst_ids=ids, dma_engine_mask=topo.mask(core, peers[0]), remote_sem=T.sem["p" + tag], srcs=[blk],
                                              dsts=[blk for c in peers])], local_sem=T.sem["l" + tag])
        ne = len(topo.engines(core, peers[0]))
        toks_all["l" + tag] = ne
        arrive("p" + tag, len(peers) * ne, [kind + x + "p"])

    def forward(x, kind, buf, w):
        pre("G", [kind + x + "o0", kind + x + "o1", kind + x + "p"], [])
        tag = buf[1] + x
        blk = T[buf][:, 4 * w * half:4 * w * half + 4 * w]
        es = topo.engines(core, mate)
        if kind + x in FREE:
            es = [e for e in es if e not in topo.engines(core, peers[0])]
        g.remote_dma(blk, blk, T.sem["m" + tag], T.sem["f" + tag], topo.addr(mate)[1], topo.addr(mate)[0], sum(1 << e for e in es))
        toks_all["f" + tag] = len(es)
        arrive("m" + tag, len(es), [kind + x + "m"])

    def have(kind, x, h):
        return [kind + x + "o0", kind + x + "o1", kind + x + "p"] if h == half else [kind + x + "m"]

    own_walls(0)
    send("0", "LW", "LW0", 128)
    flds = [("f8", 3, 31), ("f16", 4, 15), ("f31", 0, 31), ("f15", 0, 15), ("f119", 0, 119), ("f4", 2, 31)]

    def fld(n):
        j = [x[0] for x in flds].index(n)
        return T.MF[:, 128 * j:128 * j + 128]

    cp("V", T.FB[:, 0:768], T.FI[:, 0:768], ["FI%d" % j for j in range(6)], ["FB"])
    mms([(T.K0[:, 0:128], MB("ICO%d" % j) if j else MB("IB"), T.FB[:, 128 * j:128 * j + 128], j == 0, j == 5) for j in range(6)],
        ["FB", "IB"] + ["ICO%d" % j for j in range(1, 6)], ["K0.h"], ["K0"])
    cp("V", T.FB[:, 768:896], T.FI[:, 768:896], ["FI6"], ["FB6"])
    lin("OXl", "OXn", 1, 8.0, "V")
    for h in (0, 1):
        mat(MB("OXL%d" % h), "OXL%d" % h, Xm, "XI", "OXl", None, ["n0", "rho"][h])
    cp("V", T.HB[:], T.K0[:, 0:128], ["K0.h"], ["HB"], ["K0"])
    low = T.FB[:, 768:896]
    for h, bank in ((0, "RV"), (1, "NP")):
        mms([(T[bank][:, 0:128], MB("OXH%d" % h), T.HB[:], True, False), (T[bank][:, 0:128], MB("OXL%d" % h), low, False, True)],
            ["HB", "FB6", "OXH%d" % h, "OXL%d" % h], [bank + ".x"], [bank])
    for h, bank in ((0, "RV"), (1, "NP")):
        for b in (0, 1):
            c0 = 256 * me + 128 * b + 64 * h
            cp("V" if h == 0 else "S", T.LOi[:, c0:c0 + 64], T[bank][:, 64 * b:64 * b + 64], [bank + ".x"], ["LOio%d" % h + ("b" if b else "")], [bank])
    for h in (0, 1):
        wr["LOio%d" % h] = wr["LOio%d" % h] + wr["LOio%db" % h]
    own_walls(1)
    send("i", "LO", "LOi", 256)
    send("1", "LW", "LW1", 128)
    forward("0", "LW", "LW0", 128)
    forward("i", "LO", "LOi", 256)
    forward("1", "LW", "LW1", 128)
    lin("pa", "h3", -16, "X0")
    lin("pb", "rho", 8, "pa")
    lin("PERMh", "pb", 1, 16.0)
    mat(MB("PERM1"), "PERM1", Xm, "XI", "PERMh", 1.0)
    sc(MB("PERM64"), MB("PERM1"), 64.0, ["PERM1"], ["PERM64"])
    mms([(T.K1[:, 0:128], MB("PERM64"), T.HB[:], True, False), (T.K1[:, 0:128], MB("PERM1"), low, False, True)],
        ["HB", "FB6", "PERM64", "PERM1"], ["K1.o"], ["K1"])
    cp("V", T.OF[:], T.K1[:, 0:128], ["K1.o"], ["OF0", "OF1"], ["K1"])
    cp("V", T.OL[:], T.OF[:], ["OF0", "OF1"], ["OL0", "OL1"])
    for j, (n, sh, m) in enumerate(flds):
        ts(fld(n), T.MI[:], sh, A.logical_shift_right, m, A.bitwise_and, ["MI"], [n])
    for p in range(4):
        lin("kr%d" % p, "k", 1, -32.0 * p)
        mat(MB("REP%d" % p), "REP%d" % p, fld("f31"), "f31", "kr%d" % p, 1.0)
        if p >= 2:
            sc(MX("REPF%d" % p), MB("REP%d" % p), 1.0, ["REP%d" % p], ["REPF%d" % p])
    emit("V", [lambda: g.vector.memset(T.W[:, 8192:8200], -BIG)], (), ["Wz"])
    lin("sent", "h3", -128, 128.0)
    emit("V", [lambda: g.vector.memset(MB("ONES"), 1.0)], (), ["ONES"])
    ones = 128 * MATB.index("ONES")
    ts(T.OT[:, 8192:8208], T.MBF[:, ones:ones + 16], col("sent"), A.mult, None, None, ["ONES", "c_sent"], ["OTz"])
    ts(T.MK[:], T.MKI[:], col("s"), A.is_equal, None, None, ["MKI", "c_s"], ["MK"])
    lin("own15", "grp", 16, 15.0)
    lin("w64", "h3", -63, 64.0)
    mat(SL("BKO"), "BKO", Xs, "XI", "own15", None, "w64")
    lin("sa", "rho", -32, "k")
    lin("SWh", "sa", 1, 16.0)
    mat(MX("SW"), "SW", Xm, "XI", "SWh", 1.0)

    def late():
        emit("V", [lambda: g.vector.memset(T.MSL[:, 0:4], 0.0), lambda: g.vector.memset(T.MSL[:, 148:160], 0.0)], (), ["GUARD"])
        mat(SL("OWN"), "OWN", Xs, "XI", "own15", 1.0)
        lin("ot", "rho", -32, "own15")
        lin("oth15", "ot", 1, 16.0)
        mat(SL("OTH"), "OTH", Xs, "XI", "oth15", 1.0)
        sc(T.MX[:, 0:152], T.MSL[:, 0:152], 32.0, ["OWN", "GUARD"], ["MX0"])
        for j, d in enumerate(DELTA):
            k0 = 160 + 144 * SLID.index("BD%d" % j)
            tt(T.MSL[:, k0:k0 + 144], T.MX[:, 4:148], T.MSL[:, 4 - d:148 - d], A.subtract, ["MX0", "OWN", "GUARD"], ["BD%d" % j])
        lin("thr1", "b0", 1, -0.5)
        lin("thr2", "b1", 1, -0.5)
        mat(MB("E8"), "E8", fld("f8"), "f8", "blk", -2.0)
        ts(MB("GT"), Xm, col("k"), A.is_gt, None, None, ["XI", "c_k"], ["GT"])
        tt(MB("E8"), MB("E8"), MB("GT"), A.mult, ["GT"], ["E8"])
        tt(MB("YM"), MB("E8"), MB("IB"), A.add, ["E8", "IB"], ["YM"])
        lin("bf", "rho", -4, "blk")
        lin("blkf", "bf", 1, 2.0)
        lin("bl2", "blkf", 2, 0.0)
        lin("bl3", "blkf", 2, 1.0)
        mat(MX("CH0"), "CH0", fld("f4"), "f4", "bl2", 1.0)
        mat(MX("CH1"), "CH1", fld("f4"), "f4", "bl3", 1.0)
        lin("ta", "rho", -16, "X0")
        lin("T0", "ta", 1, 16.0)
        lin("T8", "ta", 1, 24.0)
        lin("g0", "h3", -1, 1.0)
        lin("a0", "g0", -BIG, 0.0)
        lin("a1", "h3", -BIG, 0.0)
        lin("temp", "i", 1024, 0.0)
        mat(MB("ENT0"), "ENT0", Xm, "XI", "T0", None, "w64")
        mat(MB("ENT1"), "ENT1", Xm, "XI", "T8", None, "w64")
        for h, gn in ((0, "g0"), (1, "h3")):
            mat(MB("ANY%d" % h), "ANY%d" % h, fld("f16"), "f16", "grp", None, "a%d" % h)
            mat(MB("KX%d" % h), "KX%d" % h, fld("f119"), "f119", "T0", None, gn)

    def late2():
        tt(MX("ISW"), MX("SW"), MB("IB"), A.add, ["SW", "IB"], ["ISW"])
        names.append("kz")
        ts(col("kz"), col("k"), 0.0, A.is_equal, -1024.0, A.mult, ["c_k"], ["c_kz"])
        ts(MB("TMN"), fld("f15"), col("kz"), A.mult, None, None, ["f15", "c_kz"], ["TMN"])
        emit("V", [lambda: g.vector.memset(T.RS[:], 0.0)], (), ["RS"])
        emit("V", [lambda: g.vector.memset(T.RS[:, 0::8], -BIG)], (), ["RS"])

    def late2s():
        sc(MB("KEEPN"), MB("IB"), -16384.0, ["IB"], ["KEEPN"])
        for h in (0, 1):
            sc(MB("KN%d" % h), MB("KX%d" % h), -256.0, ["KX%d" % h], ["KN%d" % h])
        sc(MX("NSW"), MX("SW"), -1.0, ["SW"], ["NSW"])
        sc(MB("TMP"), MB("TMN"), -1.0, ["TMN"], ["TMP"])

    def late3():
        lin("iv", "rho", -8, "OXn")
        lin("INVh", "iv", 1, 8.0)
        mat(MX("INVF"), "INVF", Xm, "XI", "INVh", 1.0)
        for j, c in enumerate([-4032.0, -768.0, 512.0, 1920.0, 64.0]):
            sc(MB("INV%d" % j), MX("INVF"), c, ["INVF"], ["INV%d" % j])

    OTALL = ["OTz"] + ["OT%d%d%d" % (b, p, h) for b in (0, 1) for p in range(4) for h in (0, 1)]
    WALL = ["Wz"] + ["W%d%d%d" % (b, p, h) + z for b in (0, 1) for p in range(4) for h in (0, 1) for z in ("", "s")]
    rb = [("UP", 0, "UPa"), ("UP", 512, "UPb"), ("YY", 0, "YY"), ("DD", 0, "DD")]
    nb = [0]

    def rep_o(x, b, h, qs):
        for p in range(4):
            buf, c0, bank = rb[nb[0] % 4]
            nb[0] += 1
            out = T[buf][:, c0:c0 + 512]
            if x == "i":
                ms = [(T[buf][:, c0 + 128 * j:c0 + 128 * j + 128], MB("REP%d" % p),
                       T.LOi[:, 256 * (4 * h + j) + 128 * b:256 * (4 * h + j) + 128 * b + 128], True, True) for j in range(4)]
            else:
                ms = [(out, MB("REP%d" % p), T["LO" + x][:, 512 * h:512 * h + 512], True, True)]
            mms(ms, have("LO", x, h) + ["REP%d" % p], [bank + ".r"], [bank])
            d0 = 4096 * b + 1024 * p + 512 * h
            cp(qs[p % len(qs)], T.OT[:, d0:d0 + 512], out, [bank + ".r"], ["OT%d%d%d" % (b, p, h)], [bank])

    def rep_w_dma(x, b, h):
        n = 4 - NREP[x][h != half]
        dmas("Y", [(T.W[32 * pp:32 * pp + 32, 4096 * b + 1024 * p + 512 * h:4096 * b + 1024 * p + 512 * h + 512],
                    T["LW" + x][32 * p:32 * p + 32, 512 * h:512 * h + 512]) for p in range(n) for pp in range(4) if pp != p],
             "dW%s%d" % (x, h), have("LW", x, h) + (have("LO", "i", half) if x == "0" else []), ["W%d%d%d" % (b, p, h) for p in range(n)])

    def rep_w_same(x, b, h, q):
        for p in range(4 - NREP[x][h != half]):
            d0 = 4096 * b + 1024 * p + 512 * h
            cp(q, T.W[32 * p:32 * p + 32, d0:d0 + 512], T["LW" + x][32 * p:32 * p + 32, 512 * h:512 * h + 512], have("LW", x, h), ["W%d%d%ds" % (b, p, h)])

    def rep_w_pe(x, b, h, q):
        for p in range(4 - NREP[x][h != half], 4):
            buf, c0, bank = rb[nb[0] % 4]
            nb[0] += 1
            out = T[buf][:, c0:c0 + 512]
            mms([(out, MX("REPF%d" % p), T["LW" + x][:, 512 * h:512 * h + 512], True, True)], have("LW", x, h) + ["REPF%d" % p], [bank + ".r"], [bank])
            d0 = 4096 * b + 1024 * p + 512 * h
            cp(q, T.W[:, d0:d0 + 512], out, [bank + ".r"], ["W%d%d%d" % (b, p, h)], [bank])

    def expand(x, b):
        for q in range(16):
            hh = q >> 3
            cp("S", T["XE%d" % b][:, q::16], T["LW" + x][:, 128 * me + 64 * hh:128 * me + 64 * hh + 64], ["LW%so%d" % (x, hh)], ["XE%d.%d" % (b, q)])

    def lists_gather(t):
        b = t & 1
        tt(T.GM[:], T.OT[:].indirect(T.OL[:, 64 * b:64 * b + 64]), T.MK[:, 16 * t:16 * t + 1024], A.mult, OTALL + ["OL%d" % b, "MK"], ["GM"])

    def lists(t):
        b = t & 1
        mms([(T.K0[:, 0:64], SL("BKO", q), T.GM[:, q::16], q == 0, q == 15) for q in range(16)], ["GM", "BKO"], ["K0.k"], ["K0"])
        ts(T.KC[:], T.K0[:, 0:64], -8192.0, A.add, None, None, ["K0.k"], ["KC"], ["K0"])
        mms([(T.K1[:, 0:64], MX("SW"), T.KC[:], True, True)], ["KC", "SW"], ["K1.k"], ["K1"])
        cp("V", T.KL[:, 0:64], T.K0[:, 0:64], ["K0.k"], ["KL0"], ["K0"])
        ts(T.HAS[:], T.OF[:, 64 * b:64 * b + 64], 8191.5, A.is_lt, None, None, ["OF%d" % b], ["HAS"])
        ts(T.KL[:, 64:128], T.K1[:, 0:64], 8192.0, A.add, None, None, ["K1.k"], ["KL1"], ["K1"])

    def fields(b):
        cp("V", T.YI[:], T.OF[:, 64 * b:64 * b + 64], ["OF%d" % b], ["YI"])
        for j, (sh, m) in enumerate([(12, 1), (10, 3), (9, 1), (7, 3), (6, 1)]):
            ts(T.YFI[:, 64 * j:64 * j + 64], T.YI[:], sh, A.logical_shift_right, m, A.bitwise_and, ["YI"], ["YFI%d" % j])
        cp("V", T.YFB[:], T.YFI[:], ["YFI%d" % j for j in range(5)], ["YFB"])

    def natural(b):
        mms([(T.YY[:, 128:192], MX("INVF"), T.OF[:, 64 * b:64 * b + 64], True, False)]
            + [(T.YY[:, 128:192], MB("INV%d" % j), T.YFB[:, 64 * j:64 * j + 64], False, j == 4) for j in range(5)],
            ["OF%d" % b, "YFB", "INVF"] + ["INV%d" % j for j in range(5)], ["YY.n"], ["YY"])
        cp("S", T["YO%d" % b][:], T.YY[:, 128:192], ["YY.n"], ["YO%d" % b], ["YY"])
        dmas("Y", [(T.yo[:, 64 * b:64 * b + 64], T["YO%d" % b][:])], "dO%d" % b, ["YO%d" % b], [])

    def round_(t):
        b, m = t & 1, 1 + t
        x = {0: "0", 1: "1", 2: "2"}[t]
        nx = {0: "2", 1: "3", 2: None}[t]
        xe = ["XE%d.%d" % (b, q) for q in range(16)]
        Wt = T.W[:]
        mine = "LW%so" % x
        ol = T.OL[:, 64 * b:64 * b + 64]
        emit("S", [lambda: g.scalar.activation(out=T.U[:], in_=Wt.indirect(ol), func=AF.Copy)], WALL + ["OL%d" % b], ["U"])
        cp("S", T.UP[:], T.U[:], ["U"], ["UPa.r", "UPb.r"], ["UPa", "UPb"])
        if t == 0:
            late2s()
        XE = T["XE%d" % b]
        tt(T.VO[:], Wt.indirect(T.KL[:, 0:64]), XE[:], A.is_gt, WALL + ["KL0"] + xe, ["VO"])
        mms([(T.RV[:, 0:64], SL("OWN", q), T.VO[:, q::16], q == 0, False) for q in range(16)], ["VO", "OWN"], ["RV.v"], ["RV"])
        tt(T.VX[:], Wt.indirect(T.KL[:, 64:128]), XE[:], A.is_lt, WALL + ["KL1"] + xe, ["VX"])
        mms([(T.RV[:, 0:64], SL("OTH", q), T.VX[:, q::16], False, q == 15) for q in range(16)], ["VX", "OTH"], ["RV.v2"], ["RV"])
        st = {1: [(0, 1, 2)], 2: [(0, 2, 4), (1, 3, 4)], 3: [(0, 3, 4), (1, 2, 4)]}[m]
        thr = "thr1" if m == 1 else "thr2"
        nq = 0
        for u, v, s in st:
            for y, z in ((u, v), (v, u)):
                tt(T.C[:, y::s], T.U[:, y::s], T.UP[:, z::s], A.is_gt, ["U", "UPa.r", "UPb.r"], ["C%d" % y], ["UPa", "UPb"])
                qs = range(y, 16, s)
                mms([(T.DD[:, 0:64], SL("BD%d" % DELTA.index((q ^ m) - q), q), T.C[:, q::16], nq + j == 0, nq + j == 15) for j, q in enumerate(qs)],
                    ["C%d" % y] + ["BD%d" % j for j in range(6)], ["DD.d%d" % y], ["DD"])
                nq += len(qs)
        dd = ["DD.d%d" % y for u, v, s in st for y in (u, v)]
        ts(T.R1[:], T.RV[:, 0:64], 1024.0, A.mult, col(thr), A.add, ["RV.v", "RV.v2", "c_" + thr], ["R1"], ["RV"])
        tt(T.REV[:], T.DD[:, 0:64], T.R1[:], A.is_ge, dd + ["R1"], ["REV"], ["DD"])
        mms([(T.YY[:, 0:64], MB("YM"), T.REV[:], True, True)], ["REV", "YM"], ["YY.y"], ["YY"])
        ts(T.ND[:], T.DD[:, 0:64], col(thr), A.is_ge, None, None, dd + ["c_" + thr], ["ND"], ["DD"])
        tt(T.NH[:], T.ND[:], T.HAS[:], A.mult, ["ND", "HAS"], ["NH"])
        ts(T.FF[:], T.YY[:, 0:64], 0.5, A.is_gt, None, None, ["YY.y"], ["FF"], ["YY"])
        tt(T.FK[:], T.FF[:], T.KC[:], A.mult, ["FF", "KC"], ["FK"])
        mms([(T.YY[:, 64:96], MX("CH%d" % e), T.FK[:, 32 * e:32 * e + 32], e == 0, e == 1) for e in (0, 1)], ["FK", "CH0", "CH1"], ["YY.c"], ["YY"])
        tt(T.KEEP[:], T.NH[:], T.FF[:], A.subtract, ["NH", "FF"], ["KEEP"])
        tt(T.OK[:], T.OF[:, 64 * b:64 * b + 64], T.KEEP[:], A.mult, ["OF%d" % b, "KEEP"], ["OK"])
        mms([(T.NP[:, 0:64], MB("KEEPN"), T.KEEP[:], True, False)], ["KEEP", "KEEPN"], ["NP.n"], ["NP"])
        ts(T.CL[:], T.YY[:, 64:96], 8192.0, A.add, None, None, ["YY.c"], ["CL"], ["YY"])
        if nx:
            mms([(T.RV[:, 64 * h + 128:64 * h + 192], MB("KX%d" % h), T.KEEP[:], True, True) for h in (0, 1)], ["KEEP", "KX0", "KX1"], ["RV.k"], ["RV"])
        emit("V", [lambda: g.vector.tensor_copy(out=T.E[:, 0:256], in_=T.OT[:].indirect(T.CL[:, 0:16]))], OTALL + ["CL"], ["E0"])
        emit("S", [lambda: g.scalar.activation(out=T.E[:, 256:512], in_=T.OT[:].indirect(T.CL[:, 16:32]), func=AF.Copy)], OTALL + ["CL"], ["E1"])
        mms([(T.NP[:, 32 * e:32 * e + 32], MB("ENT%d" % h), T.E[:, 8 * h + 4 * e::16], False, h == 1 and e == 1) for e in (0, 1) for h in (0, 1)],
            ["E0", "E1", "ENT0", "ENT1"], ["NP.n2"], ["NP"])
        if nx:
            old = T.LOi[:, 256 * me + 128 * b:256 * me + 128 * b + 128]
            tt(T.OXA[:], T.RV[:, 128:256], old, A.mult, ["RV.k", "LOio0", "LOio1"], ["OXA"], ["RV"])
            for h in (0, 1):
                mms([(T.DD[:, 128 + 64 * h:192 + 64 * h], MB("KN%d" % h), T.KEEP[:], True, False)]
                    + [(T.DD[:, 128 + 64 * h + 32 * e:160 + 64 * h + 32 * e], MB("IB"), T.E[:, 8 * h + 4 * e::16], False, e == 1) for e in (0, 1)],
                    ["KEEP", "E0", "E1", "IB", "KN%d" % h], ["DD.x%d" % h], ["DD"])
        n = T.OF[:, 64 * b:64 * b + 64]
        tt(n, T.NP[:, 0:64], T.OK[:], A.max, ["NP.n", "NP.n2", "OK"], ["OF%d" % b], ["NP"])
        cp("V", ol, n, ["OF%d" % b], ["OL%d" % b])
        for h, bank in ((0, "K0"), (1, "K1")):
            mms([(T[bank][:, 0:64], MX("NSW"), T["LW" + x][:, 128 * me + 64 * h:128 * me + 64 * h + 64], True, False),
                 (T[bank][:, 0:64], MB("TMN"), T.MBF[:, ones:ones + 64], False, False)], [mine + "0", mine + "1", "NSW", "TMN", "ONES"], [bank + ".a"], [bank])
        emit("S", [lambda: g.scalar.activation(out=T.U5[:, 384:1024], in_=Wt.indirect(T.OL[:, 64 * b + 24:64 * b + 64]), func=AF.Copy)],
             WALL + ["OL%d" % b], ["U51"])
        if nx:
            for h in (0, 1):
                tt(T["LO" + nx][:, 128 * me + 64 * h:128 * me + 64 * h + 64], T.DD[:, 128 + 64 * h:192 + 64 * h], T.OXA[:, 64 * h:64 * h + 64], A.max,
                   ["DD.x%d" % h, "OXA"], ["LO%so%d" % (nx, h)], ["DD"])
            send(nx, "LO", "LO" + nx, 128)
        emit("V", [lambda: g.vector.tensor_copy(out=T.U5[:, 0:384], in_=Wt.indirect(T.OL[:, 64 * b:64 * b + 24]))], WALL + ["OL%d" % b], ["U50"])
        ts(T.HN[:], n, 8191.5, A.is_lt, None, None, ["OF%d" % b], ["HN"])
        for h, bank in ((0, "K0"), (1, "K1")):
            mms([(T[bank][:, 0:64], MB("ANY%d" % h), T.HN[:], False, True)], ["HN", "ANY%d" % h], [bank + ".b"], [bank])
        for h, c0, c1 in ((0, 0, 384), (1, 384, 1024)):
            emit("V", [lambda: g.vector.tensor_tensor_scan(out=T.MX[:, c0:c1], data0=T.RS[:, 0:c1 - c0], data1=T.U5[:, c0:c1],
                                                           initial=-2.0 * BIG, op0=A.add, op1=A.max)], ["RS", "U5%d" % h], ["MX%d" % h])
        for h, bank in ((0, "K0"), (1, "K1")):
            tt(T.OWNW[:, 64 * h:64 * h + 64], T.MX[:, 7 + 8 * h::16], T[bank][:, 0:64], A.max, ["MX0", "MX1", bank + ".a", bank + ".b"], ["OWN%d" % h], [bank])
        mms([(T.NP[:, 256:384], MB("TMP"), MB("ONES"), True, False)], ["TMP", "ONES"], ["NP.t"], ["NP"])
        mms([(T.RV[:, 256:384], MX("ISW"), T.OWNW[:], True, True)], ["OWN0", "OWN1", "ISW"], ["RV.s"], ["RV"])
        mms([(T.NP[:, 256:384], MX("SW"), T.OWNW[:], False, True)], ["OWN0", "OWN1", "SW"], ["NP.t2"], ["NP"])
        if not nx:
            fields(b)
            natural(b)
        ts(T.M1[:], T.RV[:, 256:384], 0.0, A.min, col("n0"), A.add, ["RV.s", "c_n0"], ["M1"], ["RV"])
        ts(T.M2[:], T.M1[:], 1, A.arith_shift_right, None, None, ["M1"], ["M2"])
        if nx:
            tt(T["LW" + nx][:, 128 * me:128 * me + 128], T.M2[:], T.NP[:, 256:384], A.subtract, ["M2", "NP.t", "NP.t2"], ["LW%so0" % nx, "LW%so1" % nx], ["NP"])
            send(nx, "LW", "LW" + nx, 128)
            forward(nx, "LO", "LO" + nx, 128)
            forward(nx, "LW", "LW" + nx, 128)
            src, sr = T["LW" + nx][:, 128 * me:128 * me + 128], ["LW%so0" % nx, "LW%so1" % nx]
        else:
            tt(T.NF[:], T.M2[:], T.NP[:, 256:384], A.subtract, ["M2", "NP.t", "NP.t2"], ["NF"], ["NP"])
            src, sr = T.NF[:], ["NF"]
        if t > 0:
            ts(T["YW%d" % b][:], src, col("temp"), A.add, col("sgn"), A.mult, sr + ["c_temp", "c_sgn"], ["YW%d" % b])
            for q, y, r0 in (("Y", T.yl, 0), ("S", T.yr, 16)):
                pre(q, ["YW%d" % b], [])
                for P in range(4):
                    for h in (0, 1):
                        eng[q].dma_start(out=y[32 * P + 16 * h:32 * P + 16 * h + 16, 64 * b:64 * b + 64],
                                         in_=T["YW%d" % b][32 * P + r0:32 * P + r0 + 16, 64 * h:64 * h + 64]).then_inc(T.sem["dY%d" % b], 16)
            toks_all["dY%d" % b] = 16 * 16
            if nx:
                fields(b)
                natural(b)

    hs = [half, 1 - half]
    expand("0", 0)
    rep_w_pe("0", 0, hs[0], "S")
    late()
    for b in (0, 1):
        rep_o("i", b, hs[0], "S")
    for x, b in (("0", 0), ("1", 1)):
        for h in hs:
            rep_w_dma(x, b, h)
    rep_w_same("0", 0, hs[0], "S")
    for b in (0, 1):
        rep_o("i", b, hs[1], "VS")
    rep_w_same("0", 0, hs[1], "S")
    lists_gather(0)
    rep_w_same("1", 1, hs[0], "V")
    rep_w_pe("0", 0, hs[1], "S")
    rep_w_pe("1", 1, hs[0], "S")
    lists(0)
    rep_w_same("1", 1, hs[1], "V")
    rep_w_pe("1", 1, hs[1], "S")
    late2()
    round_(0)
    late3()
    expand("1", 1)
    for t, x, b in ((1, "2", 0), (2, "3", 1)):
        for h in hs:
            rep_w_dma(x, b, h)
        for h in hs:
            rep_o(x, b, h, "VS")
        lists_gather(t)
        rep_w_same(x, b, hs[0], "S")
        rep_w_pe(x, b, hs[0], "S")
        lists(t)
        rep_w_same(x, b, hs[1], "S")
        rep_w_pe(x, b, hs[1], "S")
        round_(t)
        if t == 1:
            expand("2", 0)
    for s in SEMAPHORES:
        if toks_all.get(s, 0) > known["G"].get(s, 0):
            g.wait_ge(T.sem[s], toks_all[s])
